import numpy as np
import ml_dtypes


def mxq(x, axis, fmt="e4m3"):
    dtype, down = {"e4m3": (ml_dtypes.float8_e4m3fn, 7), "e5m2": (ml_dtypes.float8_e5m2, 14)}[fmt]
    v = np.moveaxis(np.asarray(x, np.float32).astype(ml_dtypes.bfloat16).astype(np.float64), axis, -1)
    blocks = v.reshape(v.shape[:-1] + (-1, 32))
    amax = np.abs(blocks).max(-1, keepdims=True)
    byte = np.maximum(np.where(amax > 0, np.frexp(amax)[1] - 1 + 127, 0) - down, 1)
    scale = np.exp2(byte - 127.0)
    codes = (blocks / scale).astype(np.float32).astype(dtype).astype(np.float64)
    return np.moveaxis((codes * scale).reshape(v.shape), -1, axis)


WIDE = False


def mx_kscale(k):
    if not WIDE:
        return np.ones(k)
    levels = np.array([10, -10, 5, -5, 0])
    if k % 512:
        return np.exp2(np.random.permutation(np.resize(levels, k // 32))).repeat(32)
    a = np.empty((k // 512, 16))
    for p in range(k // 512):
        a[p, :8] = np.random.permutation(np.resize(levels, 8))
        for g in range(8):
            far = levels[np.abs(levels - a[p, g]) >= 10]
            a[p, g + 8] = far[np.random.randint(len(far))]
    return np.exp2(a.ravel()).repeat(32)


def f64(x):
    return np.asarray(x).astype(np.float64)


def striped(idx):
    return np.tile(idx.reshape(-1, 16).T, (8, 1)).astype(np.uint16)


def unstriped(offs):
    return offs[:16].T.reshape(-1).astype(np.int64)


E2M1 = np.array([0.0, 0.5, 1.0, 1.5, 2.0, 3.0, 4.0, 6.0, -0.0, -0.5, -1.0, -1.5, -2.0, -3.0, -4.0, -6.0])


def pack_weight(w, fmt):
    k, n = w.shape
    w = f64(np.asarray(w, np.float32).astype(ml_dtypes.bfloat16)).reshape(k // 32, 32, n)
    amax = np.abs(w).max(1)
    if fmt == "e4m3":
        byte = np.frexp(amax)[1] - 1 + 127 - 7
    else:
        mant, ex = np.frexp(amax / 6.0)
        byte = np.where(mant > 0.5, ex, ex - 1) + 127
    byte = np.clip(np.where(amax > 0, byte, 1), 1, 254)
    scaled = (w * np.exp2(127.0 - byte)[:, None, :]).reshape(k, n).astype(np.float32)
    by_word = np.ascontiguousarray(scaled.reshape(k // 512, 128, 4, n).transpose(0, 1, 3, 2))
    if fmt == "e4m3":
        words = by_word.astype(ml_dtypes.float8_e4m3fn).view(np.uint8)
    else:
        c = by_word.astype(ml_dtypes.float4_e2m1fn).view(np.uint8) & 0xF
        words = (c[..., 0::2] | (c[..., 1::2] << 4)).reshape(k // 512, 128, 2 * n)
    return np.ascontiguousarray(words), np.ascontiguousarray(byte.astype(np.uint8).reshape(k // 512, 16, n))


def unpack_weight(words, scales, fmt):
    g, _, n = scales.shape
    words = np.ascontiguousarray(words).reshape(g, 128, n, -1)
    if fmt == "e4m3":
        vals = words.view(ml_dtypes.float8_e4m3fn).astype(np.float64)
    else:
        nib = np.empty((g, 128, n, 4), np.uint8)
        nib[..., 0::2] = words & 0xF
        nib[..., 1::2] = words >> 4
        vals = E2M1[nib]
    vals = vals * np.repeat(np.exp2(scales.astype(np.float64) - 127.0), 8, axis=1)[..., None]
    return vals.transpose(0, 1, 3, 2).reshape(g * 512, n)


def gelu(v):
    return 0.5 * v * (1.0 + np.tanh(np.sqrt(2.0 / np.pi) * (v + 0.044715 * v**3)))


K, T, S, H, N = 1024, 4096, 1024, 512, 512

def setup_inputs():
    n = np.random.standard_normal
    s = mx_kscale(K)[:, None]
    u = mx_kscale(H)[:, None]
    tab_words, tab_scales = pack_weight(n((K, T)) * s, "e4m3")
    offs = striped(np.random.permutation(T)[:S])
    offs2 = striped(np.random.permutation(T)[:S])
    offs3 = striped(np.random.permutation(T)[:S])
    w1 = (n((K, H)) / np.sqrt(K) / s * u.T).astype(np.float32)
    w2_words, w2_scales = pack_weight(n((K, H)) / np.sqrt(K) / s * u.T, "e2m1")
    w3_words, w3_scales = pack_weight(0.4 * n((K, H)) / np.sqrt(K) / s, "e4m3")
    w4 = (0.5 * n((H, N)) / np.sqrt(H) / u).astype(np.float32)
    b = (0.3 * n(N)).astype(np.float32)
    return {"tab_words": tab_words, "tab_scales": tab_scales, "offs": offs, "offs2": offs2, "offs3": offs3,
            "w1": w1, "w2_words": w2_words, "w2_scales": w2_scales,
            "w3_words": w3_words, "w3_scales": w3_scales, "w4": w4, "b": b}

def reference(tab_words, tab_scales, offs, offs2, offs3, w1, w2_words, w2_scales, w3_words, w3_scales, w4, b):
    vc = unpack_weight(tab_words, tab_scales, "e4m3")[:, unstriped(offs)]
    vp = unpack_weight(tab_words, tab_scales, "e4m3")[:, unstriped(offs2)]
    vt = unpack_weight(tab_words, tab_scales, "e4m3")[:, unstriped(offs3)]
    w2 = unpack_weight(w2_words, w2_scales, "e2m1")
    w3 = unpack_weight(w3_words, w3_scales, "e4m3")
    col = mxq(f64(w1), 0, "e4m3").T @ vc
    pred = w2.T @ vp
    size = w3.T @ vt
    h = np.minimum(col, pred) * np.exp(size)
    y = mxq(f64(w4), 0, "e4m3").T @ mxq(h, 0, "e4m3")
    return np.exp(y + f64(b)[:, None])

@@ -1,0 +1,254 @@
+from contextlib import ExitStack
+
+import concourse.mybir as mybir
+
+K, T, S, H, N = 1024, 4096, 1024, 512, 512
+FLOPS = 2 * (3 * K * H * S + H * N * S)
+
+F32 = mybir.dt.float32
+BF16 = mybir.dt.bfloat16
+I32 = mybir.dt.int32
+U32 = mybir.dt.uint32
+U16 = mybir.dt.uint16
+U8 = mybir.dt.uint8
+FP8X4 = mybir.dt.float8_e4m3fn_x4
+FP4X4 = mybir.dt.float4_e2m1fn_x4
+EXP = mybir.ActivationFunctionType.Exp
+MIN = mybir.AluOpType.min
+MULT = mybir.AluOpType.mult
+
+P = 128
+PASSES = 2
+SLOTS = 4
+HALF = 512
+CHUNK = 128
+
+
+def tile_list_sketch_cardinality_kernel(
+    tc, tab_words, tab_scales, offs, offs2, offs3, w1, w2_words, w2_scales, w3_words, w3_scales, w4, b, out
+):
+    nc = tc.nc
+    with ExitStack() as ctx:
+        keep = ctx.enter_context(tc.tile_pool(name="keep", bufs=1))
+        ring = ctx.enter_context(tc.tile_pool(name="ring", bufs=4))
+        psum = ctx.enter_context(tc.psum_pool(name="psum", bufs=1))
+
+        def held(name, shape, dtype):
+            return keep.tile(shape, dtype, name=name, align_bytes=64)
+
+        lists = {}
+        for name, src in (("size", offs3), ("pred", offs2), ("col", offs)):
+            lists[name] = held("list_" + name, [P, S // 16], U16)
+            nc.sync.dma_start(lists[name][:], src)
+
+        scale_table = held("scale_table", [P, T // 4], I32)
+        nc.vector.memset(scale_table[:], 0)
+        w3_scale_raw = held("w3_scale_raw", [P, PASSES, H // 4], I32)
+        nc.vector.memset(w3_scale_raw[:], 0)
+        w2_scale_raw = held("w2_scale_raw", [P, PASSES, H // 4], I32)
+        nc.vector.memset(w2_scale_raw[:], 0)
+        pred_plane1 = held("pred_plane1", [P, S // 4], I32)
+        nc.vector.memset(pred_plane1[:], 0)
+
+        warm = held("warm", [P, 1], F32)
+        nc.gpsimd.memset(warm[:], 0.0)
+        warm_out = held("warm_out", [P, 1], F32)
+        nc.scalar.activation(warm_out[:], warm[:], EXP)
+
+        def load_weight_scales(queue, dst, src):
+            for q in range(4):
+                queue.dma_start(
+                    dst[32 * q : 32 * q + 4, :, :],
+                    src.bitcast(I32)[:, 4 * q : 4 * q + 4, :].rearrange("a r c -> r a c"),
+                )
+
+        tab_scale_words = tab_scales.bitcast(I32)
+        for q in range(4):
+            nc.sync.dma_start(scale_table[32 * q : 32 * q + 8, :], tab_scale_words[:, 4 * q : 4 * q + 4, :])
+        w2_raw = held("w2_raw", [P, PASSES, H // 2], I32)
+        nc.sync.dma_start(w2_raw[:], w2_words.rearrange("a p c -> p a c").bitcast(I32))
+        w3_raw = held("w3_raw", [P, PASSES, H], I32)
+        nc.sync.dma_start(w3_raw[:], w3_words.rearrange("a p c i -> p a (c i)").bitcast(I32))
+        load_weight_scales(nc.sync, w3_scale_raw, w3_scales)
+
+        word_table = []
+        for a in range(PASSES):
+            word_table.append(held("word_table%d" % a, [P, T], I32))
+            nc.sync.dma_start(word_table[a][:], tab_words[a].rearrange("p t i -> p (t i)").bitcast(I32))
+        load_weight_scales(nc.sync, w2_scale_raw, w2_scales)
+        w1_raw = []
+        for a in range(PASSES):
+            w1_raw.append(held("w1_raw%d" % a, [P, SLOTS, H], F32))
+            nc.sync.dma_start(w1_raw[a][:], w1[512 * a : 512 * (a + 1), :].rearrange("(p s) c -> p s c", s=SLOTS))
+        w4_raw = held("w4_raw", [P, SLOTS, N], F32)
+        w4_rows = w4.rearrange("(g t i) n -> t g i n", t=SLOTS, i=8)
+        for t in range(SLOTS):
+            nc.sync.dma_start(w4_raw[:, t, :], w4_rows[t])
+        bias = held("bias", [P, N // P], F32)
+        with nc.allow_non_contiguous_dma(reason="one bias value a partition"):
+            nc.sync.dma_start(bias[:], b.rearrange("(t p) -> p t", p=P))
+
+        def permuted(name, raw, run):
+            dst = held(name, [P, SLOTS, PASSES, 16 * run], I32)
+            nc.vector.tensor_copy(
+                dst[:].rearrange("p t a (g i) -> p t (a g) i", i=run),
+                raw[:].rearrange("p a (g t i) -> p t (a g) i", t=SLOTS, i=run),
+            )
+            return dst
+
+
+        planes = {}
+
+        def gather_scales(name, tag):
+            planes[name] = keep.tile([P, S], U8, name="plane_" + name, tag=tag, align_bytes=64)
+            nc.vector.tensor_copy(planes[name][:], scale_table[:].bitcast(U8).indirect(lists[name][:]))
+
+        gather_scales("size", "plane_size")
+        gather_scales("pred", "plane_pred")
+        for r in range(4):
+            nc.scalar.dma_start(pred_plane1[r:P:32, :], planes["pred"][:].bitcast(I32)[4 + r : P : 32, :])
+        w2_codes = permuted("w2_codes", w2_raw, 4)
+        w3_codes = permuted("w3_codes", w3_raw, 8)
+        w3_planes = permuted("w3_planes", w3_scale_raw, 2)
+        w2_planes = permuted("w2_planes", w2_scale_raw, 2)
+
+        words = {}
+        reused = {("size", 1, 0): "words_size01", ("pred", 1, 0): "words_pred00"}
+
+        def gather_words(name, half, a):
+            label = "words_%s%d%d" % (name, half, a)
+            dst = keep.tile([P, HALF], U32, name=label, tag=reused.get((name, half, a), label), align_bytes=64)
+            cols = slice(half * HALF // 16, (half + 1) * HALF // 16)
+            nc.vector.tensor_copy(dst[:], word_table[a][:].bitcast(U32).indirect(lists[name][:, cols]))
+            words[name, half, a] = dst
+
+        w1_codes, w1_scales = [], []
+
+        def group_w1(a):
+            grouped = held("w1_grouped%d" % a, [P, SLOTS, 16, 8, SLOTS], BF16)
+            src = w1_raw[a][:].rearrange("p s (g t i) -> p t g i s", t=SLOTS, i=8)
+            for t in range(SLOTS):
+                nc.scalar.copy(grouped[:, t], src[:, t])
+            return grouped
+
+        def quantize(name, grouped_flat, width):
+            codes = held(name + "_codes", [P, width], U32)
+            scales = held(name + "_scales", [P, width], U8)
+            nc.vector.quantize_mx(out=codes[:].bitcast(FP8X4), scales=scales[:], in_=grouped_flat)
+            return codes, scales
+
+        def stationary(name, a, t):
+            if name == "size":
+                return w3_codes[:, t, a, :].bitcast(FP8X4), w3_planes[:, t, a, :].bitcast(U8)
+            if name == "pred":
+                return w2_codes[:, t, a, :].bitcast(U8).bitcast(FP4X4), w2_planes[:, t, a, :].bitcast(U8)
+            cols = slice(t * P, (t + 1) * P)
+            return w1_codes[a][:, cols].bitcast(FP8X4), w1_scales[a][:, cols]
+
+        def moving_scale(name, a, cols):
+            if name == "pred" and a == 1:
+                return pred_plane1[:].bitcast(U8)[:, cols]
+            return planes[name][4 * a : P, cols]
+
+        def product(name, chunk):
+            bank = psum.tile([P, SLOTS, CHUNK], F32, name="first", bufs=6)
+            half, c0 = divmod(chunk * CHUNK, HALF)
+            for t in range(SLOTS):
+                for a in range(PASSES):
+                    codes, scale = stationary(name, a, t)
+                    nc.tensor.matmul_mx(
+                        out=bank[:, t, :],
+                        lhsT=codes,
+                        lhsT_scale=scale,
+                        rhs=words[name, half, a][:, c0 : c0 + CHUNK].bitcast(FP8X4),
+                        rhs_scale=moving_scale(name, a, slice(chunk * CHUNK, (chunk + 1) * CHUNK)),
+                        start=(a == 0),
+                        stop=(a == PASSES - 1),
+                    )
+            return bank[:].rearrange("p t j -> p j t")
+
+        factor, pred = {}, {}
+
+        def size_chunks(chunks):
+            for chunk in chunks:
+                factor[chunk] = held("factor%d" % chunk, [P, CHUNK, SLOTS], F32)
+                nc.scalar.activation(factor[chunk][:], product("size", chunk), EXP)
+
+        def pred_chunks(chunks):
+            for chunk in chunks:
+                pred[chunk] = held("pred%d" % chunk, [P, CHUNK, SLOTS], F32)
+                nc.scalar.copy(pred[chunk][:], product("pred", chunk))
+
+        out_view = out.rearrange("(t p) j -> p t j", p=P)
+        w4_q = []
+
+        def make_h(chunks):
+            h = ring.tile([P, len(chunks), CHUNK, SLOTS], BF16, name="h", align_bytes=64)
+            smaller = {}
+            for chunk in chunks:
+                smaller[chunk] = ring.tile([P, CHUNK, SLOTS], F32, name="smaller")
+                nc.vector.tensor_tensor(smaller[chunk][:], product("col", chunk), pred[chunk][:], MIN)
+            for u, chunk in enumerate(chunks):
+                nc.vector.tensor_tensor(h[:, u], smaller[chunk][:], factor[chunk][:], MULT)
+            return h
+
+        def head(first_chunk, h_part):
+            width = h_part.shape[1] * CHUNK
+            j0 = first_chunk * CHUNK
+            codes, scales = quantize("h%d" % first_chunk, h_part.rearrange("p u j t -> p (u j t)"), width)
+            w4_codes, w4_scales = w4_q
+            for pair in range(2):
+                bank = psum.tile([P, 2, width], F32, name="second", bufs=2)
+                result = ring.tile([P, 2, width], F32, name="result")
+                for u in range(2):
+                    cols = slice((2 * pair + u) * P, (2 * pair + u + 1) * P)
+                    nc.tensor.matmul_mx(
+                        out=bank[:, u, :],
+                        lhsT=w4_codes[:, cols].bitcast(FP8X4),
+                        lhsT_scale=w4_scales[:, cols],
+                        rhs=codes[:].bitcast(FP8X4),
+                        rhs_scale=scales[:],
+                        start=True,
+                        stop=True,
+                    )
+                for u in range(2):
+                    tile_n = 2 * pair + u
+                    nc.scalar.activation(result[:, u, :], bank[:, u, :], EXP, bias=bias[:, tile_n : tile_n + 1])
+                nc.sync.dma_start(out_view[:, 2 * pair : 2 * pair + 2, j0 : j0 + width], result[:])
+
+        gather_words("size", 0, 0)
+        gather_words("size", 0, 1)
+        size_chunks(range(0, 4))
+        gather_words("pred", 0, 0)
+        gather_words("pred", 0, 1)
+        w1_grouped = [group_w1(a) for a in range(PASSES)]
+        pred_chunks(range(0, 4))
+        gather_words("size", 1, 0)
+        gather_words("size", 1, 1)
+        gather_scales("col", "words_size00")
+        gather_words("col", 0, 0)
+        gather_words("col", 0, 1)
+        for a in range(PASSES):
+            codes, scales = quantize("w1_%d" % a, w1_grouped[a][:].rearrange("p t g i s -> p (t g i s)"), H)
+            w1_codes.append(codes)
+            w1_scales.append(scales)
+        gather_words("pred", 1, 0)
+        gather_words("pred", 1, 1)
+        gather_words("col", 1, 0)
+        gather_words("col", 1, 1)
+        size_chunks((4, 5))
+        h0 = make_h((0, 1))
+        pred_chunks((4, 5))
+        h1 = make_h((2, 3))
+        w4_grouped = held("w4_grouped", [P, N, SLOTS], BF16)
+        nc.scalar.copy(w4_grouped[:], w4_raw[:].rearrange("p t n -> p n t"))
+        w4_q.extend(quantize("w4", w4_grouped[:].rearrange("p n t -> p (n t)"), N))
+        size_chunks((6, 7))
+        h2 = make_h((4, 5))
+        pred_chunks((6, 7))
+        head(0, h0[:])
+        head(2, h1[:])
+        h3 = make_h((6, 7))
+        head(4, h2[:])
+        head(6, h3[:, 0:1])
+        head(7, h3[:, 1:2])

@@ -16,12 +16,16 @@ FP4X4 = mybir.dt.float4_e2m1fn_x4
 EXP = mybir.ActivationFunctionType.Exp
 MIN = mybir.AluOpType.min
 MULT = mybir.AluOpType.mult
+ADD = mybir.AluOpType.add
 
 P = 128
 PASSES = 2
 SLOTS = 4
 HALF = 512
 CHUNK = 128
+FIRST_BANKS = 5
+SECOND_BANKS = 3
+REUSED = {'w2_planes': 'w3_raw', 'words_size10': 'words_size00', 'words_col00': 'words_size01', 'w1_raw0': 'pred0', 'words_pred11': 'scale_table', 'words_col01': 'smaller3', 'w4_grouped': 'factor0', 'words_col10': 'w1_raw1', 'words_pred10': 'w1_grouped1', 'words_pred00': 'pred1'}
 
 
 def tile_list_sketch_cardinality_kernel(
@@ -30,128 +34,124 @@ def tile_list_sketch_cardinality_kernel(
     nc = tc.nc
     with ExitStack() as ctx:
         keep = ctx.enter_context(tc.tile_pool(name="keep", bufs=1))
-        ring = ctx.enter_context(tc.tile_pool(name="ring", bufs=4))
         psum = ctx.enter_context(tc.psum_pool(name="psum", bufs=1))
+        tiles = {}
 
         def held(name, shape, dtype):
-            return keep.tile(shape, dtype, name=name, align_bytes=64)
+            tiles[name] = keep.tile(shape, dtype, name=name, tag=REUSED.get(name, name), align_bytes=64)
+            return tiles[name]
 
-        lists = {}
-        for name, src in (("size", offs3), ("pred", offs2), ("col", offs)):
-            lists[name] = held("list_" + name, [P, S // 16], U16)
-            nc.sync.dma_start(lists[name][:], src)
+        def load_list(name, src):
+            nc.sync.dma_start(held("list_" + name, [P, S // 16], U16)[:], src)
 
-        scale_table = held("scale_table", [P, T // 4], I32)
-        nc.vector.memset(scale_table[:], 0)
-        w3_scale_raw = held("w3_scale_raw", [P, PASSES, H // 4], I32)
-        nc.vector.memset(w3_scale_raw[:], 0)
-        w2_scale_raw = held("w2_scale_raw", [P, PASSES, H // 4], I32)
-        nc.vector.memset(w2_scale_raw[:], 0)
-        pred_plane1 = held("pred_plane1", [P, S // 4], I32)
-        nc.vector.memset(pred_plane1[:], 0)
+        def zeroed(engine, name, shape):
+            engine.memset(held(name, shape, I32)[:], 0)
 
-        warm = held("warm", [P, 1], F32)
-        nc.gpsimd.memset(warm[:], 0.0)
-        warm_out = held("warm_out", [P, 1], F32)
-        nc.scalar.activation(warm_out[:], warm[:], EXP)
+        def warm_up():
+            warm = held("warm", [P, 1], F32)
+            nc.gpsimd.memset(warm[:], 0.0)
+            nc.scalar.activation(held("warm_out", [P, 1], F32)[:], warm[:], EXP)
 
-        def load_weight_scales(queue, dst, src):
+        def load_table_scales():
+            src = tab_scales.bitcast(I32)
+            for q in range(4):
+                nc.sync.dma_start(tiles["scale_table"][32 * q : 32 * q + 8, :], src[:, 4 * q : 4 * q + 4, :])
+
+        def load_weight_scales(queue, name, src):
             for q in range(4):
                 queue.dma_start(
-                    dst[32 * q : 32 * q + 4, :, :],
+                    tiles[name][32 * q : 32 * q + 4, :, :],
                     src.bitcast(I32)[:, 4 * q : 4 * q + 4, :].rearrange("a r c -> r a c"),
                 )
 
-        tab_scale_words = tab_scales.bitcast(I32)
-        for q in range(4):
-            nc.sync.dma_start(scale_table[32 * q : 32 * q + 8, :], tab_scale_words[:, 4 * q : 4 * q + 4, :])
-        w2_raw = held("w2_raw", [P, PASSES, H // 2], I32)
-        nc.sync.dma_start(w2_raw[:], w2_words.rearrange("a p c -> p a c").bitcast(I32))
-        w3_raw = held("w3_raw", [P, PASSES, H], I32)
-        nc.sync.dma_start(w3_raw[:], w3_words.rearrange("a p c i -> p a (c i)").bitcast(I32))
-        load_weight_scales(nc.sync, w3_scale_raw, w3_scales)
+        def load_w2():
+            nc.sync.dma_start(held("w2_raw", [P, PASSES, H // 2], I32)[:], w2_words.rearrange("a p c -> p a c").bitcast(I32))
 
-        word_table = []
-        for a in range(PASSES):
-            word_table.append(held("word_table%d" % a, [P, T], I32))
-            nc.sync.dma_start(word_table[a][:], tab_words[a].rearrange("p t i -> p (t i)").bitcast(I32))
-        load_weight_scales(nc.sync, w2_scale_raw, w2_scales)
-        w1_raw = []
-        for a in range(PASSES):
-            w1_raw.append(held("w1_raw%d" % a, [P, SLOTS, H], F32))
-            nc.sync.dma_start(w1_raw[a][:], w1[512 * a : 512 * (a + 1), :].rearrange("(p s) c -> p s c", s=SLOTS))
-        w4_raw = held("w4_raw", [P, SLOTS, N], F32)
-        w4_rows = w4.rearrange("(g t i) n -> t g i n", t=SLOTS, i=8)
-        for t in range(SLOTS):
-            nc.sync.dma_start(w4_raw[:, t, :], w4_rows[t])
-        bias = held("bias", [P, N // P], F32)
-        with nc.allow_non_contiguous_dma(reason="one bias value a partition"):
-            nc.sync.dma_start(bias[:], b.rearrange("(t p) -> p t", p=P))
+        def load_w3():
+            nc.sync.dma_start(held("w3_raw", [P, PASSES, H], I32)[:], w3_words.rearrange("a p c i -> p a (c i)").bitcast(I32))
 
-        def permuted(name, raw, run):
+        def load_table(a):
+            nc.sync.dma_start(held("word_table%d" % a, [P, T], I32)[:], tab_words[a].rearrange("p t i -> p (t i)").bitcast(I32))
+
+        def load_w1(a):
+            rows = w1[512 * a : 512 * (a + 1), :].rearrange("(p s) c -> p s c", s=SLOTS)
+            nc.sync.dma_start(held("w1_raw%d" % a, [P, SLOTS, H], F32)[:], rows)
+
+        def load_w4():
+            raw = held("w4_raw", [P, SLOTS, N], F32)
+            rows = w4.rearrange("(g t i) n -> t g i n", t=SLOTS, i=8)
+            for t in range(SLOTS):
+                nc.sync.dma_start(raw[:, t, :], rows[t])
+
+        def load_bias():
+            with nc.allow_non_contiguous_dma(reason="one bias value a partition"):
+                nc.sync.dma_start(held("bias", [P, N // P], F32)[:], b.rearrange("(t p) -> p t", p=P))
+
+        def permute(name, raw, run):
             dst = held(name, [P, SLOTS, PASSES, 16 * run], I32)
             nc.vector.tensor_copy(
                 dst[:].rearrange("p t a (g i) -> p t (a g) i", i=run),
-                raw[:].rearrange("p a (g t i) -> p t (a g) i", t=SLOTS, i=run),
+                tiles[raw][:].rearrange("p a (g t i) -> p t (a g) i", t=SLOTS, i=run),
             )
-            return dst
 
+        def gather_scales(name):
+            window = tiles["scale_table"][:].bitcast(U8)
+            nc.vector.tensor_copy(held("plane_" + name, [P, S], U8)[:], window.indirect(tiles["list_" + name][:]))
 
-        planes = {}
-
-        def gather_scales(name, tag):
-            planes[name] = keep.tile([P, S], U8, name="plane_" + name, tag=tag, align_bytes=64)
-            nc.vector.tensor_copy(planes[name][:], scale_table[:].bitcast(U8).indirect(lists[name][:]))
-
-        gather_scales("size", "plane_size")
-        gather_scales("pred", "plane_pred")
-        for r in range(4):
-            nc.scalar.dma_start(pred_plane1[r:P:32, :], planes["pred"][:].bitcast(I32)[4 + r : P : 32, :])
-        w2_codes = permuted("w2_codes", w2_raw, 4)
-        w3_codes = permuted("w3_codes", w3_raw, 8)
-        w3_planes = permuted("w3_planes", w3_scale_raw, 2)
-        w2_planes = permuted("w2_planes", w2_scale_raw, 2)
-
-        words = {}
-        reused = {("size", 1, 0): "words_size01", ("pred", 1, 0): "words_pred00"}
+        def shift_pred_plane():
+            src = tiles["plane_pred"][:].bitcast(I32)
+            for r in range(4):
+                nc.scalar.dma_start(tiles["pred_plane1"][r:P:32, :], src[4 + r : P : 32, :])
 
         def gather_words(name, half, a):
-            label = "words_%s%d%d" % (name, half, a)
-            dst = keep.tile([P, HALF], U32, name=label, tag=reused.get((name, half, a), label), align_bytes=64)
+            dst = held("words_%s%d%d" % (name, half, a), [P, HALF], U32)
             cols = slice(half * HALF // 16, (half + 1) * HALF // 16)
-            nc.vector.tensor_copy(dst[:], word_table[a][:].bitcast(U32).indirect(lists[name][:, cols]))
-            words[name, half, a] = dst
+            window = tiles["word_table%d" % a][:].bitcast(U32)
+            nc.vector.tensor_copy(dst[:], window.indirect(tiles["list_" + name][:, cols]))
 
-        w1_codes, w1_scales = [], []
+        def pool_round(dst, src):
+            nc.gpsimd.tensor_scalar(dst, src, 1.0, 0.0, MULT, ADD)
 
-        def group_w1(a):
+        def group_w1(engine_copy, a):
             grouped = held("w1_grouped%d" % a, [P, SLOTS, 16, 8, SLOTS], BF16)
-            src = w1_raw[a][:].rearrange("p s (g t i) -> p t g i s", t=SLOTS, i=8)
+            src = tiles["w1_raw%d" % a][:].rearrange("p s (g t i) -> p t g i s", t=SLOTS, i=8)
             for t in range(SLOTS):
-                nc.scalar.copy(grouped[:, t], src[:, t])
-            return grouped
+                engine_copy(grouped[:, t], src[:, t])
 
-        def quantize(name, grouped_flat, width):
+        def group_w4(engine_copy):
+            grouped = held("w4_grouped", [P, N, SLOTS], BF16)
+            src = tiles["w4_raw"][:].rearrange("p t n -> p n t")
+            for n0 in range(0, N, P):
+                engine_copy(grouped[:, n0 : n0 + P, :], src[:, n0 : n0 + P, :])
+
+        def quantize(name, grouped_flat):
+            width = grouped_flat.shape[1] // SLOTS
             codes = held(name + "_codes", [P, width], U32)
             scales = held(name + "_scales", [P, width], U8)
             nc.vector.quantize_mx(out=codes[:].bitcast(FP8X4), scales=scales[:], in_=grouped_flat)
             return codes, scales
 
+        def quantize_w1(a):
+            quantize("w1_%d" % a, tiles["w1_grouped%d" % a][:].rearrange("p t g i s -> p (t g i s)"))
+
+        def quantize_w4():
+            quantize("w4", tiles["w4_grouped"][:].rearrange("p n t -> p (n t)"))
+
         def stationary(name, a, t):
             if name == "size":
-                return w3_codes[:, t, a, :].bitcast(FP8X4), w3_planes[:, t, a, :].bitcast(U8)
+                return tiles["w3_codes"][:, t, a, :].bitcast(FP8X4), tiles["w3_planes"][:, t, a, :].bitcast(U8)
             if name == "pred":
-                return w2_codes[:, t, a, :].bitcast(U8).bitcast(FP4X4), w2_planes[:, t, a, :].bitcast(U8)
+                return tiles["w2_codes"][:, t, a, :].bitcast(U8).bitcast(FP4X4), tiles["w2_planes"][:, t, a, :].bitcast(U8)
             cols = slice(t * P, (t + 1) * P)
-            return w1_codes[a][:, cols].bitcast(FP8X4), w1_scales[a][:, cols]
+            return tiles["w1_%d_codes" % a][:, cols].bitcast(FP8X4), tiles["w1_%d_scales" % a][:, cols]
 
         def moving_scale(name, a, cols):
             if name == "pred" and a == 1:
-                return pred_plane1[:].bitcast(U8)[:, cols]
-            return planes[name][4 * a : P, cols]
+                return tiles["pred_plane1"][:].bitcast(U8)[:, cols]
+            return tiles["plane_" + name][4 * a : P, cols]
 
         def product(name, chunk):
-            bank = psum.tile([P, SLOTS, CHUNK], F32, name="first", bufs=6)
+            bank = psum.tile([P, SLOTS, CHUNK], F32, name="first", bufs=FIRST_BANKS)
             half, c0 = divmod(chunk * CHUNK, HALF)
             for t in range(SLOTS):
                 for a in range(PASSES):
@@ -160,95 +160,134 @@ def tile_list_sketch_cardinality_kernel(
                         out=bank[:, t, :],
                         lhsT=codes,
                         lhsT_scale=scale,
-                        rhs=words[name, half, a][:, c0 : c0 + CHUNK].bitcast(FP8X4),
+                        rhs=tiles["words_%s%d%d" % (name, half, a)][:, c0 : c0 + CHUNK].bitcast(FP8X4),
                         rhs_scale=moving_scale(name, a, slice(chunk * CHUNK, (chunk + 1) * CHUNK)),
                         start=(a == 0),
                         stop=(a == PASSES - 1),
                     )
             return bank[:].rearrange("p t j -> p j t")
 
-        factor, pred = {}, {}
+        def size(chunk):
+            nc.scalar.activation(held("factor%d" % chunk, [P, CHUNK, SLOTS], F32)[:], product("size", chunk), EXP)
 
-        def size_chunks(chunks):
-            for chunk in chunks:
-                factor[chunk] = held("factor%d" % chunk, [P, CHUNK, SLOTS], F32)
-                nc.scalar.activation(factor[chunk][:], product("size", chunk), EXP)
+        def pred(chunk):
+            nc.scalar.copy(held("pred%d" % chunk, [P, CHUNK, SLOTS], F32)[:], product("pred", chunk))
 
-        def pred_chunks(chunks):
-            for chunk in chunks:
-                pred[chunk] = held("pred%d" % chunk, [P, CHUNK, SLOTS], F32)
-                nc.scalar.copy(pred[chunk][:], product("pred", chunk))
+        def smaller(chunk):
+            dst = held("smaller%d" % chunk, [P, CHUNK, SLOTS], F32)
+            nc.vector.tensor_tensor(dst[:], product("col", chunk), tiles["pred%d" % chunk][:], MIN)
+
+        def times(engine, chunk):
+            pair = "h%d" % (chunk // 2)
+            if pair not in tiles:
+                held(pair, [P, 2, CHUNK, SLOTS], BF16)
+            engine.tensor_tensor(tiles[pair][:, chunk % 2], tiles["smaller%d" % chunk][:], tiles["factor%d" % chunk][:], MULT)
 
         out_view = out.rearrange("(t p) j -> p t j", p=P)
-        w4_q = []
 
-        def make_h(chunks):
-            h = ring.tile([P, len(chunks), CHUNK, SLOTS], BF16, name="h", align_bytes=64)
-            smaller = {}
-            for chunk in chunks:
-                smaller[chunk] = ring.tile([P, CHUNK, SLOTS], F32, name="smaller")
-                nc.vector.tensor_tensor(smaller[chunk][:], product("col", chunk), pred[chunk][:], MIN)
-            for u, chunk in enumerate(chunks):
-                nc.vector.tensor_tensor(h[:, u], smaller[chunk][:], factor[chunk][:], MULT)
-            return h
-
-        def head(first_chunk, h_part):
-            width = h_part.shape[1] * CHUNK
-            j0 = first_chunk * CHUNK
-            codes, scales = quantize("h%d" % first_chunk, h_part.rearrange("p u j t -> p (u j t)"), width)
-            w4_codes, w4_scales = w4_q
-            for pair in range(2):
-                bank = psum.tile([P, 2, width], F32, name="second", bufs=2)
-                result = ring.tile([P, 2, width], F32, name="result")
-                for u in range(2):
-                    cols = slice((2 * pair + u) * P, (2 * pair + u + 1) * P)
+        def head(chunk, count):
+            width = count * CHUNK
+            j0 = chunk * CHUNK
+            h_part = tiles["h%d" % (chunk // 2)][:, chunk % 2 : chunk % 2 + count]
+            codes, scales = quantize("hq%d" % chunk, h_part.rearrange("p u j t -> p (u j t)"))
+            group = HALF // width if 0 else 2
+            for n0 in range(0, N // P, group):
+                bank = psum.tile([P, group, width], F32, name="second", bufs=SECOND_BANKS)
+                result = held("result%d_%d" % (chunk, n0), [P, group, width], F32)
+                for u in range(group):
+                    cols = slice((n0 + u) * P, (n0 + u + 1) * P)
                     nc.tensor.matmul_mx(
                         out=bank[:, u, :],
-                        lhsT=w4_codes[:, cols].bitcast(FP8X4),
-                        lhsT_scale=w4_scales[:, cols],
+                        lhsT=tiles["w4_codes"][:, cols].bitcast(FP8X4),
+                        lhsT_scale=tiles["w4_scales"][:, cols],
                         rhs=codes[:].bitcast(FP8X4),
                         rhs_scale=scales[:],
                         start=True,
                         stop=True,
                     )
-                for u in range(2):
-                    tile_n = 2 * pair + u
-                    nc.scalar.activation(result[:, u, :], bank[:, u, :], EXP, bias=bias[:, tile_n : tile_n + 1])
-                nc.sync.dma_start(out_view[:, 2 * pair : 2 * pair + 2, j0 : j0 + width], result[:])
+                for u in range(group):
+                    nc.scalar.activation(result[:, u, :], bank[:, u, :], EXP, bias=tiles["bias"][:, n0 + u : n0 + u + 1])
+                nc.sync.dma_start(out_view[:, n0 : n0 + group, j0 : j0 + width], result[:])
 
-        gather_words("size", 0, 0)
+        load_list("size", offs3)
+        load_list("pred", offs2)
+        load_list("col", offs)
+        warm_up()
+        zeroed(nc.vector, "w3_scale_raw", [P, PASSES, H // 4])
+        zeroed(nc.vector, "scale_table", [P, T // 4])
+        load_table_scales()
+        load_w2()
+        zeroed(nc.gpsimd, "w2_scale_raw", [P, PASSES, H // 4])
+        load_weight_scales(nc.sync, "w3_scale_raw", w3_scales)
+        load_w3()
+        load_table(0)
+        load_table(1)
+        gather_scales("size")
         gather_words("size", 0, 1)
-        size_chunks(range(0, 4))
-        gather_words("pred", 0, 0)
-        gather_words("pred", 0, 1)
-        w1_grouped = [group_w1(a) for a in range(PASSES)]
-        pred_chunks(range(0, 4))
-        gather_words("size", 1, 0)
-        gather_words("size", 1, 1)
-        gather_scales("col", "words_size00")
-        gather_words("col", 0, 0)
+        permute("w3_planes", "w3_scale_raw", 2)
+        load_w1(0)
+        gather_scales("pred")
         gather_words("col", 0, 1)
-        for a in range(PASSES):
-            codes, scales = quantize("w1_%d" % a, w1_grouped[a][:].rearrange("p t g i s -> p (t g i s)"), H)
-            w1_codes.append(codes)
-            w1_scales.append(scales)
+        gather_words("size", 0, 0)
+        permute("w2_codes", "w2_raw", 4)
+        zeroed(nc.vector, "pred_plane1", [P, S // 4])
+        permute("w3_codes", "w3_raw", 8)
+        group_w1(pool_round, 0)
+        shift_pred_plane()
+        load_w1(1)
+        size(1)
+        size(2)
+        load_bias()
+        size(0)
+        load_weight_scales(nc.gpsimd, "w2_scale_raw", w2_scales)
+        gather_words("pred", 0, 0)
+        group_w1(nc.scalar.copy, 1)
+        permute("w2_planes", "w2_scale_raw", 2)
+        gather_words("pred", 0, 1)
+        pred(2)
+        size(3)
+        gather_words("size", 1, 1)
+        gather_words("size", 1, 0)
+        quantize_w1(1)
+        gather_words("col", 0, 0)
+        pred(3)
+        pred(0)
+        gather_words("col", 1, 1)
+        gather_scales("col")
+        quantize_w1(0)
+        size(4)
+        pred(1)
+        smaller(0)
+        smaller(1)
+        smaller(2)
+        times(nc.gpsimd, 2)
         gather_words("pred", 1, 0)
+        size(7)
         gather_words("pred", 1, 1)
         gather_words("col", 1, 0)
-        gather_words("col", 1, 1)
-        size_chunks((4, 5))
-        h0 = make_h((0, 1))
-        pred_chunks((4, 5))
-        h1 = make_h((2, 3))
-        w4_grouped = held("w4_grouped", [P, N, SLOTS], BF16)
-        nc.scalar.copy(w4_grouped[:], w4_raw[:].rearrange("p t n -> p n t"))
-        w4_q.extend(quantize("w4", w4_grouped[:].rearrange("p n t -> p (n t)"), N))
-        size_chunks((6, 7))
-        h2 = make_h((4, 5))
-        pred_chunks((6, 7))
-        head(0, h0[:])
-        head(2, h1[:])
-        h3 = make_h((6, 7))
-        head(4, h2[:])
-        head(6, h3[:, 0:1])
-        head(7, h3[:, 1:2])
+        load_w4()
+        smaller(3)
+        size(5)
+        times(nc.vector, 1)
+        times(nc.vector, 3)
+        pred(5)
+        pred(4)
+        smaller(5)
+        times(nc.gpsimd, 0)
+        group_w4(nc.scalar.copy)
+        size(6)
+        pred(6)
+        smaller(4)
+        times(nc.gpsimd, 5)
+        pred(7)
+        quantize_w4()
+        smaller(6)
+        times(nc.vector, 6)
+        times(nc.vector, 4)
+        head(2, 2)
+        head(0, 2)
+        smaller(7)
+        head(4, 2)
+        head(6, 1)
+        times(nc.vector, 7)
+        head(7, 1)

@@ -23,9 +23,12 @@ PASSES = 2
 SLOTS = 4
 HALF = 512
 CHUNK = 128
-FIRST_BANKS = 5
-SECOND_BANKS = 3
-REUSED = {'w2_planes': 'w3_raw', 'words_size10': 'words_size00', 'words_col00': 'words_size01', 'w1_raw0': 'pred0', 'words_pred11': 'scale_table', 'words_col01': 'smaller3', 'w4_grouped': 'factor0', 'words_col10': 'w1_raw1', 'words_pred10': 'w1_grouped1', 'words_pred00': 'pred1'}
+CHUNKS = HALF // CHUNK
+FIRST_BANKS = 6
+SECOND_BANKS = 2
+SCALE_ROW0 = 96
+LISTS = ("size", "pred", "col")
+POOL_CHUNKS = 5
 
 
 def tile_list_sketch_cardinality_kernel(
@@ -37,31 +40,29 @@ def tile_list_sketch_cardinality_kernel(
         psum = ctx.enter_context(tc.psum_pool(name="psum", bufs=1))
         tiles = {}
 
-        def held(name, shape, dtype):
-            tiles[name] = keep.tile(shape, dtype, name=name, tag=REUSED.get(name, name), align_bytes=64)
+        def held(name, shape, dtype, tag=None):
+            tiles[name] = keep.tile(shape, dtype, name=name, tag=tag or name, align_bytes=64)
             return tiles[name]
 
         def load_list(name, src):
             nc.sync.dma_start(held("list_" + name, [P, S // 16], U16)[:], src)
 
-        def zeroed(engine, name, shape):
-            engine.memset(held(name, shape, I32)[:], 0)
-
-        def warm_up():
-            warm = held("warm", [P, 1], F32)
-            nc.gpsimd.memset(warm[:], 0.0)
-            nc.scalar.activation(held("warm_out", [P, 1], F32)[:], warm[:], EXP)
-
         def load_table_scales():
-            src = tab_scales.bitcast(I32)
-            for q in range(4):
-                nc.sync.dma_start(tiles["scale_table"][32 * q : 32 * q + 8, :], src[:, 4 * q : 4 * q + 4, :])
+            window = held("scale_table", [P, T // 4], I32)
+            nc.sync.dma_start(window[SCALE_ROW0:P, :], tab_scales.bitcast(I32).rearrange("a q c -> (a q) c"))
+            nc.vector.memset(window[0:SCALE_ROW0, :], 0)
 
-        def load_weight_scales(queue, name, src):
+        def load_weight_scales():
+            w3_raw = held("w3_scale_raw", [P, 1, H // 4], I32)
+            w2_raw = held("w2_scale_raw", [P, PASSES, H // 4], I32)
+            nc.gpsimd.memset(w3_raw[:], 0)
+            nc.gpsimd.memset(w2_raw[:], 0)
             for q in range(4):
-                queue.dma_start(
-                    tiles[name][32 * q : 32 * q + 4, :, :],
-                    src.bitcast(I32)[:, 4 * q : 4 * q + 4, :].rearrange("a r c -> r a c"),
+                nc.gpsimd.dma_start(w3_raw[32 * q : 32 * q + 8, 0, :], w3_scales.bitcast(I32)[:, 4 * q : 4 * q + 4, :])
+            for q in range(4):
+                nc.gpsimd.dma_start(
+                    w2_raw[32 * q : 32 * q + 4, :, :],
+                    w2_scales.bitcast(I32)[:, 4 * q : 4 * q + 4, :].rearrange("a r c -> r a c"),
                 )
 
         def load_w2():
@@ -87,24 +88,31 @@ def tile_list_sketch_cardinality_kernel(
             with nc.allow_non_contiguous_dma(reason="one bias value a partition"):
                 nc.sync.dma_start(held("bias", [P, N // P], F32)[:], b.rearrange("(t p) -> p t", p=P))
 
-        def permute(name, raw, run):
-            dst = held(name, [P, SLOTS, PASSES, 16 * run], I32)
-            nc.vector.tensor_copy(
+        def permute(name, raw, run, rows):
+            dst = held(name, [P, SLOTS, rows, 16 * run], I32)
+            nc.gpsimd.tensor_copy(
                 dst[:].rearrange("p t a (g i) -> p t (a g) i", i=run),
                 tiles[raw][:].rearrange("p a (g t i) -> p t (a g) i", t=SLOTS, i=run),
             )
 
-        def gather_scales(name):
+        def gather_scales():
             window = tiles["scale_table"][:].bitcast(U8)
-            nc.vector.tensor_copy(held("plane_" + name, [P, S], U8)[:], window.indirect(tiles["list_" + name][:]))
+            picked = held("picked_scales", [P, len(LISTS) * S], U8)
+            for u, name in enumerate(LISTS):
+                nc.vector.tensor_copy(picked[:, u * S : (u + 1) * S], window.indirect(tiles["list_" + name][:]))
 
-        def shift_pred_plane():
-            src = tiles["plane_pred"][:].bitcast(I32)
-            for r in range(4):
-                nc.scalar.dma_start(tiles["pred_plane1"][r:P:32, :], src[4 + r : P : 32, :])
+        def clear_planes():
+            for a in range(PASSES):
+                nc.vector.memset(held("plane%d" % a, [P, len(LISTS) * S // 4], I32)[:], 0)
+
+        def place_planes(a):
+            src = tiles["picked_scales"][:].bitcast(I32)
+            for q in range(4):
+                row = SCALE_ROW0 + 16 * a + 4 * q
+                nc.sync.dma_start(tiles["plane%d" % a][32 * q : 32 * q + 4, :], src[row : row + 4, :])
 
         def gather_words(name, half, a):
-            dst = held("words_%s%d%d" % (name, half, a), [P, HALF], U32)
+            dst = held("words_%s%d%d" % (name, half, a), [P, HALF], U32, tag="words_%s%d" % (name, a))
             cols = slice(half * HALF // 16, (half + 1) * HALF // 16)
             window = tiles["word_table%d" % a][:].bitcast(U32)
             nc.vector.tensor_copy(dst[:], window.indirect(tiles["list_" + name][:, cols]))
@@ -139,31 +147,27 @@ def tile_list_sketch_cardinality_kernel(
 
         def stationary(name, a, t):
             if name == "size":
-                return tiles["w3_codes"][:, t, a, :].bitcast(FP8X4), tiles["w3_planes"][:, t, a, :].bitcast(U8)
+                return tiles["w3_codes"][:, t, a, :].bitcast(FP8X4), tiles["w3_planes"][4 * a : P, t, 0, :].bitcast(U8)
             if name == "pred":
                 return tiles["w2_codes"][:, t, a, :].bitcast(U8).bitcast(FP4X4), tiles["w2_planes"][:, t, a, :].bitcast(U8)
             cols = slice(t * P, (t + 1) * P)
             return tiles["w1_%d_codes" % a][:, cols].bitcast(FP8X4), tiles["w1_%d_scales" % a][:, cols]
 
-        def moving_scale(name, a, cols):
-            if name == "pred" and a == 1:
-                return tiles["pred_plane1"][:].bitcast(U8)[:, cols]
-            return tiles["plane_" + name][4 * a : P, cols]
-
         def product(name, chunk):
             bank = psum.tile([P, SLOTS, CHUNK], F32, name="first", bufs=FIRST_BANKS)
             half, c0 = divmod(chunk * CHUNK, HALF)
-            for t in range(SLOTS):
-                for a in range(PASSES):
+            j0 = LISTS.index(name) * S + chunk * CHUNK
+            for a in range(PASSES):
+                for t in range(SLOTS):
                     codes, scale = stationary(name, a, t)
                     nc.tensor.matmul_mx(
                         out=bank[:, t, :],
                         lhsT=codes,
                         lhsT_scale=scale,
                         rhs=tiles["words_%s%d%d" % (name, half, a)][:, c0 : c0 + CHUNK].bitcast(FP8X4),
-                        rhs_scale=moving_scale(name, a, slice(chunk * CHUNK, (chunk + 1) * CHUNK)),
-                        start=(a == 0),
-                        stop=(a == PASSES - 1),
+                        rhs_scale=tiles["plane%d" % a][:].bitcast(U8)[:, j0 : j0 + CHUNK],
+                        start=(a == 0 and t == 0),
+                        stop=(a == PASSES - 1 and t == SLOTS - 1),
                     )
             return bank[:].rearrange("p t j -> p j t")
 
@@ -177,7 +181,8 @@ def tile_list_sketch_cardinality_kernel(
             dst = held("smaller%d" % chunk, [P, CHUNK, SLOTS], F32)
             nc.vector.tensor_tensor(dst[:], product("col", chunk), tiles["pred%d" % chunk][:], MIN)
 
-        def times(engine, chunk):
+        def times(chunk):
+            engine = nc.gpsimd if chunk < POOL_CHUNKS else nc.vector
             pair = "h%d" % (chunk // 2)
             if pair not in tiles:
                 held(pair, [P, 2, CHUNK, SLOTS], BF16)
@@ -190,7 +195,7 @@ def tile_list_sketch_cardinality_kernel(
             j0 = chunk * CHUNK
             h_part = tiles["h%d" % (chunk // 2)][:, chunk % 2 : chunk % 2 + count]
             codes, scales = quantize("hq%d" % chunk, h_part.rearrange("p u j t -> p (u j t)"))
-            group = HALF // width if 0 else 2
+            group = 2
             for n0 in range(0, N // P, group):
                 bank = psum.tile([P, group, width], F32, name="second", bufs=SECOND_BANKS)
                 result = held("result%d_%d" % (chunk, n0), [P, group, width], F32)
@@ -209,85 +214,47 @@ def tile_list_sketch_cardinality_kernel(
                     nc.scalar.activation(result[:, u, :], bank[:, u, :], EXP, bias=tiles["bias"][:, n0 + u : n0 + u + 1])
                 nc.sync.dma_start(out_view[:, n0 : n0 + group, j0 : j0 + width], result[:])
 
+        load_table_scales()
         load_list("size", offs3)
         load_list("pred", offs2)
         load_list("col", offs)
-        warm_up()
-        zeroed(nc.vector, "w3_scale_raw", [P, PASSES, H // 4])
-        zeroed(nc.vector, "scale_table", [P, T // 4])
-        load_table_scales()
-        load_w2()
-        zeroed(nc.gpsimd, "w2_scale_raw", [P, PASSES, H // 4])
-        load_weight_scales(nc.sync, "w3_scale_raw", w3_scales)
-        load_w3()
+        load_weight_scales()
+        clear_planes()
         load_table(0)
+        load_w3()
+        load_w2()
         load_table(1)
-        gather_scales("size")
-        gather_words("size", 0, 1)
-        permute("w3_planes", "w3_scale_raw", 2)
+        gather_scales()
+        place_planes(0)
         load_w1(0)
-        gather_scales("pred")
-        gather_words("col", 0, 1)
-        gather_words("size", 0, 0)
-        permute("w2_codes", "w2_raw", 4)
-        zeroed(nc.vector, "pred_plane1", [P, S // 4])
-        permute("w3_codes", "w3_raw", 8)
-        group_w1(pool_round, 0)
-        shift_pred_plane()
+        place_planes(1)
         load_w1(1)
-        size(1)
-        size(2)
-        load_bias()
-        size(0)
-        load_weight_scales(nc.gpsimd, "w2_scale_raw", w2_scales)
-        gather_words("pred", 0, 0)
-        group_w1(nc.scalar.copy, 1)
-        permute("w2_planes", "w2_scale_raw", 2)
-        gather_words("pred", 0, 1)
-        pred(2)
-        size(3)
-        gather_words("size", 1, 1)
-        gather_words("size", 1, 0)
-        quantize_w1(1)
-        gather_words("col", 0, 0)
-        pred(3)
-        pred(0)
-        gather_words("col", 1, 1)
-        gather_scales("col")
-        quantize_w1(0)
-        size(4)
-        pred(1)
-        smaller(0)
-        smaller(1)
-        smaller(2)
-        times(nc.gpsimd, 2)
-        gather_words("pred", 1, 0)
-        size(7)
-        gather_words("pred", 1, 1)
-        gather_words("col", 1, 0)
         load_w4()
-        smaller(3)
-        size(5)
-        times(nc.vector, 1)
-        times(nc.vector, 3)
-        pred(5)
-        pred(4)
-        smaller(5)
-        times(nc.gpsimd, 0)
+        load_bias()
+
+        permute("w3_codes", "w3_raw", 8, PASSES)
+        permute("w3_planes", "w3_scale_raw", 2, 1)
+        permute("w2_codes", "w2_raw", 4, PASSES)
+        permute("w2_planes", "w2_scale_raw", 2, PASSES)
+        for a in range(PASSES):
+            group_w1(pool_round, a)
+            quantize_w1(a)
+        for half in range(2):
+            chunks = range(half * CHUNKS, (half + 1) * CHUNKS)
+            for a in range(PASSES):
+                for name in LISTS:
+                    gather_words(name, half, a)
+            for chunk in chunks:
+                size(chunk)
+            for chunk in chunks:
+                pred(chunk)
+            for chunk in chunks:
+                smaller(chunk)
+                times(chunk)
         group_w4(nc.scalar.copy)
-        size(6)
-        pred(6)
-        smaller(4)
-        times(nc.gpsimd, 5)
-        pred(7)
         quantize_w4()
-        smaller(6)
-        times(nc.vector, 6)
-        times(nc.vector, 4)
-        head(2, 2)
         head(0, 2)
-        smaller(7)
+        head(2, 2)
         head(4, 2)
         head(6, 1)
-        times(nc.vector, 7)
         head(7, 1)

@@ -24,11 +24,15 @@ SLOTS = 4
 HALF = 512
 CHUNK = 128
 CHUNKS = HALF // CHUNK
-FIRST_BANKS = 6
-SECOND_BANKS = 2
+FIRST_BANKS = 5
+SECOND_BANKS = 3
 SCALE_ROW0 = 96
 LISTS = ("size", "pred", "col")
-POOL_CHUNKS = 5
+W3_COL = len(LISTS) * S
+W2_COL = W3_COL + H
+PLANE = W2_COL + H
+ROWS = (PASSES + 1) * SLOTS * H
+POOL_CHUNKS = 4
 
 
 def tile_list_sketch_cardinality_kernel(
@@ -37,11 +41,17 @@ def tile_list_sketch_cardinality_kernel(
     nc = tc.nc
     with ExitStack() as ctx:
         keep = ctx.enter_context(tc.tile_pool(name="keep", bufs=1))
+        shared = ctx.enter_context(tc.tile_pool(name="shared", bufs=1))
         psum = ctx.enter_context(tc.psum_pool(name="psum", bufs=1))
         tiles = {}
+        opened = []
 
         def held(name, shape, dtype, tag=None):
             tiles[name] = keep.tile(shape, dtype, name=name, tag=tag or name, align_bytes=64)
+            return tiles[name]
+
+        def placed(name, shape, dtype, offset):
+            tiles[name] = shared.tile(shape, dtype, name=name, tag=name, align_bytes=64, offset=offset)
             return tiles[name]
 
         def load_list(name, src):
@@ -52,18 +62,15 @@ def tile_list_sketch_cardinality_kernel(
             nc.sync.dma_start(window[SCALE_ROW0:P, :], tab_scales.bitcast(I32).rearrange("a q c -> (a q) c"))
             nc.vector.memset(window[0:SCALE_ROW0, :], 0)
 
-        def load_weight_scales():
-            w3_raw = held("w3_scale_raw", [P, 1, H // 4], I32)
-            w2_raw = held("w2_scale_raw", [P, PASSES, H // 4], I32)
-            nc.gpsimd.memset(w3_raw[:], 0)
-            nc.gpsimd.memset(w2_raw[:], 0)
-            for q in range(4):
-                nc.gpsimd.dma_start(w3_raw[32 * q : 32 * q + 8, 0, :], w3_scales.bitcast(I32)[:, 4 * q : 4 * q + 4, :])
-            for q in range(4):
-                nc.gpsimd.dma_start(
-                    w2_raw[32 * q : 32 * q + 4, :, :],
-                    w2_scales.bitcast(I32)[:, 4 * q : 4 * q + 4, :].rearrange("a r c -> r a c"),
-                )
+        def load_weight_scales(name, src):
+            raw = held(name, [P, H // 4], I32)
+            nc.sync.dma_start(raw[SCALE_ROW0:P, :], src.bitcast(I32).rearrange("a q c -> (a q) c"))
+
+        def stage_weight_scales(name, col0):
+            nc.gpsimd.tensor_copy(
+                tiles["staged"][SCALE_ROW0:P, col0 : col0 + H // 4].rearrange("p (t g i) -> p t g i", t=SLOTS, i=2),
+                tiles[name][SCALE_ROW0:P, :].rearrange("p (g t i) -> p t g i", t=SLOTS, i=2),
+            )
 
         def load_w2():
             nc.sync.dma_start(held("w2_raw", [P, PASSES, H // 2], I32)[:], w2_words.rearrange("a p c -> p a c").bitcast(I32))
@@ -74,19 +81,27 @@ def tile_list_sketch_cardinality_kernel(
         def load_table(a):
             nc.sync.dma_start(held("word_table%d" % a, [P, T], I32)[:], tab_words[a].rearrange("p t i -> p (t i)").bitcast(I32))
 
+        def staged_rows(u):
+            if "rows" not in tiles:
+                held("rows", [P, ROWS + N // P], F32, tag="w3_raw")
+            return tiles["rows"][:, u * SLOTS * H : (u + 1) * SLOTS * H].rearrange("p (s c) -> p s c", s=SLOTS)
+
+        def bias():
+            return tiles["rows"][:, ROWS : ROWS + N // P]
+
         def load_w1(a):
             rows = w1[512 * a : 512 * (a + 1), :].rearrange("(p s) c -> p s c", s=SLOTS)
-            nc.sync.dma_start(held("w1_raw%d" % a, [P, SLOTS, H], F32)[:], rows)
+            nc.sync.dma_start(staged_rows(a), rows)
 
         def load_w4():
-            raw = held("w4_raw", [P, SLOTS, N], F32)
+            raw = staged_rows(PASSES)
             rows = w4.rearrange("(g t i) n -> t g i n", t=SLOTS, i=8)
             for t in range(SLOTS):
                 nc.sync.dma_start(raw[:, t, :], rows[t])
 
         def load_bias():
             with nc.allow_non_contiguous_dma(reason="one bias value a partition"):
-                nc.sync.dma_start(held("bias", [P, N // P], F32)[:], b.rearrange("(t p) -> p t", p=P))
+                nc.sync.dma_start(bias(), b.rearrange("(t p) -> p t", p=P))
 
         def permute(name, raw, run, rows):
             dst = held(name, [P, SLOTS, rows, 16 * run], I32)
@@ -100,19 +115,21 @@ def tile_list_sketch_cardinality_kernel(
             picked = held("picked_scales", [P, len(LISTS) * S], U8)
             for u, name in enumerate(LISTS):
                 nc.vector.tensor_copy(picked[:, u * S : (u + 1) * S], window.indirect(tiles["list_" + name][:]))
+            staged = held("staged", [P, PLANE // 4], I32)
+            nc.vector.tensor_copy(staged[SCALE_ROW0:P, 0 : W3_COL // 4], picked[:].bitcast(I32)[SCALE_ROW0:P, :])
 
         def clear_planes():
             for a in range(PASSES):
-                nc.vector.memset(held("plane%d" % a, [P, len(LISTS) * S // 4], I32)[:], 0)
+                nc.gpsimd.memset(held("plane%d" % a, [P, PLANE // 4], I32)[:], 0)
 
         def place_planes(a):
-            src = tiles["picked_scales"][:].bitcast(I32)
-            for q in range(4):
-                row = SCALE_ROW0 + 16 * a + 4 * q
-                nc.sync.dma_start(tiles["plane%d" % a][32 * q : 32 * q + 4, :], src[row : row + 4, :])
+            src = tiles["staged"]
+            for r in range(4):
+                row = SCALE_ROW0 + 16 * a
+                nc.scalar.dma_start(tiles["plane%d" % a][r:P:32, :], src[row + r : row + 16 : 4, :])
 
         def gather_words(name, half, a):
-            dst = held("words_%s%d%d" % (name, half, a), [P, HALF], U32, tag="words_%s%d" % (name, a))
+            dst = held("words_%s%d%d" % (name, half, a), [P, HALF], U32, tag={"col10": "words_col00", "col11": "words_col01", "size10": "w2_raw", "pred10": "staged"}.get("%s%d%d" % (name, half, a)))
             cols = slice(half * HALF // 16, (half + 1) * HALF // 16)
             window = tiles["word_table%d" % a][:].bitcast(U32)
             nc.vector.tensor_copy(dst[:], window.indirect(tiles["list_" + name][:, cols]))
@@ -122,19 +139,20 @@ def tile_list_sketch_cardinality_kernel(
 
         def group_w1(engine_copy, a):
             grouped = held("w1_grouped%d" % a, [P, SLOTS, 16, 8, SLOTS], BF16)
-            src = tiles["w1_raw%d" % a][:].rearrange("p s (g t i) -> p t g i s", t=SLOTS, i=8)
+            src = staged_rows(a).rearrange("p s (g t i) -> p t g i s", t=SLOTS, i=8)
             for t in range(SLOTS):
-                engine_copy(grouped[:, t], src[:, t])
+                copy = engine_copy
+                copy(grouped[:, t], src[:, t])
 
         def group_w4(engine_copy):
             grouped = held("w4_grouped", [P, N, SLOTS], BF16)
-            src = tiles["w4_raw"][:].rearrange("p t n -> p n t")
+            src = staged_rows(PASSES).rearrange("p t n -> p n t")
             for n0 in range(0, N, P):
                 engine_copy(grouped[:, n0 : n0 + P, :], src[:, n0 : n0 + P, :])
 
-        def quantize(name, grouped_flat):
+        def quantize(name, grouped_flat, reuse=None):
             width = grouped_flat.shape[1] // SLOTS
-            codes = held(name + "_codes", [P, width], U32)
+            codes = held(name + "_codes", [P, width], U32, tag=reuse)
             scales = held(name + "_scales", [P, width], U8)
             nc.vector.quantize_mx(out=codes[:].bitcast(FP8X4), scales=scales[:], in_=grouped_flat)
             return codes, scales
@@ -143,18 +161,22 @@ def tile_list_sketch_cardinality_kernel(
             quantize("w1_%d" % a, tiles["w1_grouped%d" % a][:].rearrange("p t g i s -> p (t g i s)"))
 
         def quantize_w4():
-            quantize("w4", tiles["w4_grouped"][:].rearrange("p n t -> p (n t)"))
+            quantize("w4", tiles["w4_grouped"][:].rearrange("p n t -> p (n t)"), "pred3")
+
+        def plane(a, col0):
+            return tiles["plane%d" % a][:].bitcast(U8)[:, col0 : col0 + P]
 
         def stationary(name, a, t):
             if name == "size":
-                return tiles["w3_codes"][:, t, a, :].bitcast(FP8X4), tiles["w3_planes"][4 * a : P, t, 0, :].bitcast(U8)
+                return tiles["w3_codes"][:, t, a, :].bitcast(FP8X4), plane(a, W3_COL + t * P)
             if name == "pred":
-                return tiles["w2_codes"][:, t, a, :].bitcast(U8).bitcast(FP4X4), tiles["w2_planes"][:, t, a, :].bitcast(U8)
+                return tiles["w2_codes"][:, t, a, :].bitcast(U8).bitcast(FP4X4), plane(a, W2_COL + t * P)
             cols = slice(t * P, (t + 1) * P)
             return tiles["w1_%d_codes" % a][:, cols].bitcast(FP8X4), tiles["w1_%d_scales" % a][:, cols]
 
         def product(name, chunk):
-            bank = psum.tile([P, SLOTS, CHUNK], F32, name="first", bufs=FIRST_BANKS)
+            bank = psum.tile([P, SLOTS, CHUNK], F32, name="first", tag="first%d" % (len(opened) % FIRST_BANKS))
+            opened.append(name)
             half, c0 = divmod(chunk * CHUNK, HALF)
             j0 = LISTS.index(name) * S + chunk * CHUNK
             for a in range(PASSES):
@@ -165,7 +187,7 @@ def tile_list_sketch_cardinality_kernel(
                         lhsT=codes,
                         lhsT_scale=scale,
                         rhs=tiles["words_%s%d%d" % (name, half, a)][:, c0 : c0 + CHUNK].bitcast(FP8X4),
-                        rhs_scale=tiles["plane%d" % a][:].bitcast(U8)[:, j0 : j0 + CHUNK],
+                        rhs_scale=plane(a, j0),
                         start=(a == 0 and t == 0),
                         stop=(a == PASSES - 1 and t == SLOTS - 1),
                     )
@@ -211,50 +233,62 @@ def tile_list_sketch_cardinality_kernel(
                         stop=True,
                     )
                 for u in range(group):
-                    nc.scalar.activation(result[:, u, :], bank[:, u, :], EXP, bias=tiles["bias"][:, n0 + u : n0 + u + 1])
+                    nc.scalar.activation(result[:, u, :], bank[:, u, :], EXP, bias=bias()[:, n0 + u : n0 + u + 1])
                 nc.sync.dma_start(out_view[:, n0 : n0 + group, j0 : j0 + width], result[:])
 
         load_table_scales()
         load_list("size", offs3)
         load_list("pred", offs2)
         load_list("col", offs)
-        load_weight_scales()
         clear_planes()
+        load_weight_scales("w3_scale_raw", w3_scales)
+        load_weight_scales("w2_scale_raw", w2_scales)
         load_table(0)
         load_w3()
-        load_w2()
         load_table(1)
+        load_w2()
         gather_scales()
+        stage_weight_scales("w3_scale_raw", W3_COL // 4)
+        stage_weight_scales("w2_scale_raw", W2_COL // 4)
         place_planes(0)
-        load_w1(0)
         place_planes(1)
+        load_w1(0)
         load_w1(1)
         load_w4()
         load_bias()
 
         permute("w3_codes", "w3_raw", 8, PASSES)
-        permute("w3_planes", "w3_scale_raw", 2, 1)
         permute("w2_codes", "w2_raw", 4, PASSES)
-        permute("w2_planes", "w2_scale_raw", 2, PASSES)
+        for name in LISTS:
+            for a in range(PASSES):
+                gather_words(name, 0, a)
+        for name in LISTS[:2]:
+            for a in range(PASSES):
+                gather_words(name, 1, a)
         for a in range(PASSES):
             group_w1(pool_round, a)
             quantize_w1(a)
-        for half in range(2):
-            chunks = range(half * CHUNKS, (half + 1) * CHUNKS)
-            for a in range(PASSES):
-                for name in LISTS:
-                    gather_words(name, half, a)
-            for chunk in chunks:
-                size(chunk)
-            for chunk in chunks:
-                pred(chunk)
-            for chunk in chunks:
-                smaller(chunk)
-                times(chunk)
+
+        first, second = range(CHUNKS), range(CHUNKS, 2 * CHUNKS)
+        for chunk in first:
+            size(chunk)
+        for chunk in first:
+            pred(chunk)
+        for chunk in second:
+            size(chunk)
         group_w4(nc.scalar.copy)
+        for chunk in first:
+            smaller(chunk)
+            times(chunk)
+        for chunk in second:
+            pred(chunk)
+        for a in range(PASSES):
+            gather_words("col", 1, a)
         quantize_w4()
+        for chunk in second:
+            smaller(chunk)
         head(0, 2)
         head(2, 2)
-        head(4, 2)
-        head(6, 1)
-        head(7, 1)
+        for chunk in second:
+            times(chunk)
+            head(chunk, 1)

@@ -31,7 +31,8 @@ LISTS = ("size", "pred", "col")
 W3_COL = len(LISTS) * S
 W2_COL = W3_COL + H
 PLANE = W2_COL + H
-ROWS = (PASSES + 1) * SLOTS * H
+AFTER_W1 = ("words_size10", "words_pred10")
+REUSED = {"words_pred11": "w1_raw1", "words_col10": "pred2", "words_col11": "pred3"}
 POOL_CHUNKS = 4
 
 
@@ -81,31 +82,23 @@ def tile_list_sketch_cardinality_kernel(
         def load_table(a):
             nc.sync.dma_start(held("word_table%d" % a, [P, T], I32)[:], tab_words[a].rearrange("p t i -> p (t i)").bitcast(I32))
 
-        def staged_rows(u):
-            if "rows" not in tiles:
-                held("rows", [P, ROWS + N // P], F32, tag="w3_raw")
-            return tiles["rows"][:, u * SLOTS * H : (u + 1) * SLOTS * H].rearrange("p (s c) -> p s c", s=SLOTS)
-
-        def bias():
-            return tiles["rows"][:, ROWS : ROWS + N // P]
-
         def load_w1(a):
             rows = w1[512 * a : 512 * (a + 1), :].rearrange("(p s) c -> p s c", s=SLOTS)
-            nc.sync.dma_start(staged_rows(a), rows)
+            nc.sync.dma_start(held("w1_raw%d" % a, [P, SLOTS, H], F32)[:], rows)
 
         def load_w4():
-            raw = staged_rows(PASSES)
+            raw = held("w4_raw", [P, SLOTS, N], F32)
             rows = w4.rearrange("(g t i) n -> t g i n", t=SLOTS, i=8)
             for t in range(SLOTS):
                 nc.sync.dma_start(raw[:, t, :], rows[t])
 
         def load_bias():
             with nc.allow_non_contiguous_dma(reason="one bias value a partition"):
-                nc.sync.dma_start(bias(), b.rearrange("(t p) -> p t", p=P))
+                nc.sync.dma_start(held("bias", [P, N // P], F32)[:], b.rearrange("(t p) -> p t", p=P))
 
-        def permute(name, raw, run, rows):
+        def permute(engine, name, raw, run, rows):
             dst = held(name, [P, SLOTS, rows, 16 * run], I32)
-            nc.gpsimd.tensor_copy(
+            engine.tensor_copy(
                 dst[:].rearrange("p t a (g i) -> p t (a g) i", i=run),
                 tiles[raw][:].rearrange("p a (g t i) -> p t (a g) i", t=SLOTS, i=run),
             )
@@ -115,7 +108,7 @@ def tile_list_sketch_cardinality_kernel(
             picked = held("picked_scales", [P, len(LISTS) * S], U8)
             for u, name in enumerate(LISTS):
                 nc.vector.tensor_copy(picked[:, u * S : (u + 1) * S], window.indirect(tiles["list_" + name][:]))
-            staged = held("staged", [P, PLANE // 4], I32)
+            staged = placed("staged", [P, PLANE // 4], I32, 0)
             nc.vector.tensor_copy(staged[SCALE_ROW0:P, 0 : W3_COL // 4], picked[:].bitcast(I32)[SCALE_ROW0:P, :])
 
         def clear_planes():
@@ -129,7 +122,11 @@ def tile_list_sketch_cardinality_kernel(
                 nc.scalar.dma_start(tiles["plane%d" % a][r:P:32, :], src[row + r : row + 16 : 4, :])
 
         def gather_words(name, half, a):
-            dst = held("words_%s%d%d" % (name, half, a), [P, HALF], U32, tag={"col10": "words_col00", "col11": "words_col01", "size10": "w2_raw", "pred10": "staged"}.get("%s%d%d" % (name, half, a)))
+            label = "words_%s%d%d" % (name, half, a)
+            if label in AFTER_W1:
+                dst = placed(label, [P, HALF], U32, 4 * HALF * AFTER_W1.index(label))
+            else:
+                dst = held(label, [P, HALF], U32, tag=REUSED.get(label))
             cols = slice(half * HALF // 16, (half + 1) * HALF // 16)
             window = tiles["word_table%d" % a][:].bitcast(U32)
             nc.vector.tensor_copy(dst[:], window.indirect(tiles["list_" + name][:, cols]))
@@ -139,20 +136,20 @@ def tile_list_sketch_cardinality_kernel(
 
         def group_w1(engine_copy, a):
             grouped = held("w1_grouped%d" % a, [P, SLOTS, 16, 8, SLOTS], BF16)
-            src = staged_rows(a).rearrange("p s (g t i) -> p t g i s", t=SLOTS, i=8)
+            src = tiles["w1_raw%d" % a][:].rearrange("p s (g t i) -> p t g i s", t=SLOTS, i=8)
             for t in range(SLOTS):
-                copy = engine_copy
+                copy = nc.scalar.copy if a == 1 and t < 2 else engine_copy
                 copy(grouped[:, t], src[:, t])
 
         def group_w4(engine_copy):
             grouped = held("w4_grouped", [P, N, SLOTS], BF16)
-            src = staged_rows(PASSES).rearrange("p t n -> p n t")
+            src = tiles["w4_raw"][:].rearrange("p t n -> p n t")
             for n0 in range(0, N, P):
                 engine_copy(grouped[:, n0 : n0 + P, :], src[:, n0 : n0 + P, :])
 
-        def quantize(name, grouped_flat, reuse=None):
+        def quantize(name, grouped_flat):
             width = grouped_flat.shape[1] // SLOTS
-            codes = held(name + "_codes", [P, width], U32, tag=reuse)
+            codes = held(name + "_codes", [P, width], U32)
             scales = held(name + "_scales", [P, width], U8)
             nc.vector.quantize_mx(out=codes[:].bitcast(FP8X4), scales=scales[:], in_=grouped_flat)
             return codes, scales
@@ -161,7 +158,7 @@ def tile_list_sketch_cardinality_kernel(
             quantize("w1_%d" % a, tiles["w1_grouped%d" % a][:].rearrange("p t g i s -> p (t g i s)"))
 
         def quantize_w4():
-            quantize("w4", tiles["w4_grouped"][:].rearrange("p n t -> p (n t)"), "pred3")
+            quantize("w4", tiles["w4_grouped"][:].rearrange("p n t -> p (n t)"))
 
         def plane(a, col0):
             return tiles["plane%d" % a][:].bitcast(U8)[:, col0 : col0 + P]
@@ -199,9 +196,9 @@ def tile_list_sketch_cardinality_kernel(
         def pred(chunk):
             nc.scalar.copy(held("pred%d" % chunk, [P, CHUNK, SLOTS], F32)[:], product("pred", chunk))
 
-        def smaller(chunk):
-            dst = held("smaller%d" % chunk, [P, CHUNK, SLOTS], F32)
-            nc.vector.tensor_tensor(dst[:], product("col", chunk), tiles["pred%d" % chunk][:], MIN)
+        def smaller(chunk, col):
+            dst = held("smaller%d" % chunk, [P, CHUNK, SLOTS], F32, tag=None)
+            nc.vector.tensor_tensor(dst[:], col, tiles["pred%d" % chunk][:], MIN)
 
         def times(chunk):
             engine = nc.gpsimd if chunk < POOL_CHUNKS else nc.vector
@@ -233,7 +230,7 @@ def tile_list_sketch_cardinality_kernel(
                         stop=True,
                     )
                 for u in range(group):
-                    nc.scalar.activation(result[:, u, :], bank[:, u, :], EXP, bias=bias()[:, n0 + u : n0 + u + 1])
+                    nc.scalar.activation(result[:, u, :], bank[:, u, :], EXP, bias=tiles["bias"][:, n0 + u : n0 + u + 1])
                 nc.sync.dma_start(out_view[:, n0 : n0 + group, j0 : j0 + width], result[:])
 
         load_table_scales()
@@ -243,33 +240,33 @@ def tile_list_sketch_cardinality_kernel(
         clear_planes()
         load_weight_scales("w3_scale_raw", w3_scales)
         load_weight_scales("w2_scale_raw", w2_scales)
-        load_table(0)
         load_w3()
-        load_table(1)
         load_w2()
+        load_table(0)
+        load_table(1)
         gather_scales()
         stage_weight_scales("w3_scale_raw", W3_COL // 4)
         stage_weight_scales("w2_scale_raw", W2_COL // 4)
         place_planes(0)
         place_planes(1)
+        permute(nc.vector, "w3_codes", "w3_raw", 8, PASSES)
+        permute(nc.vector, "w2_codes", "w2_raw", 4, PASSES)
         load_w1(0)
         load_w1(1)
         load_w4()
         load_bias()
 
-        permute("w3_codes", "w3_raw", 8, PASSES)
-        permute("w2_codes", "w2_raw", 4, PASSES)
+        first, second = range(CHUNKS), range(CHUNKS, 2 * CHUNKS)
         for name in LISTS:
             for a in range(PASSES):
                 gather_words(name, 0, a)
-        for name in LISTS[:2]:
-            for a in range(PASSES):
-                gather_words(name, 1, a)
+        for a in range(PASSES):
+            gather_words("size", 1, a)
+        gather_words("pred", 1, 0)
         for a in range(PASSES):
             group_w1(pool_round, a)
             quantize_w1(a)
-
-        first, second = range(CHUNKS), range(CHUNKS, 2 * CHUNKS)
+        gather_words("pred", 1, 1)
         for chunk in first:
             size(chunk)
         for chunk in first:
@@ -278,17 +275,19 @@ def tile_list_sketch_cardinality_kernel(
             size(chunk)
         group_w4(nc.scalar.copy)
         for chunk in first:
-            smaller(chunk)
+            smaller(chunk, product("col", chunk))
             times(chunk)
         for chunk in second:
             pred(chunk)
         for a in range(PASSES):
             gather_words("col", 1, a)
+        cols = [product("col", chunk) for chunk in second]
         quantize_w4()
-        for chunk in second:
-            smaller(chunk)
         head(0, 2)
         head(2, 2)
+        smaller(CHUNKS, cols[0])
         for chunk in second:
+            if chunk + 1 in second:
+                smaller(chunk + 1, cols[chunk + 1 - CHUNKS])
             times(chunk)
             head(chunk, 1)

@@ -19,21 +19,21 @@ MULT = mybir.AluOpType.mult
 ADD = mybir.AluOpType.add
 
 P = 128
-PASSES = 2
+PASSES = K // 512
 SLOTS = 4
-HALF = 512
+RUN = 8
+BLOCKS = 16
+HALF = S // 2
 CHUNK = 128
 CHUNKS = HALF // CHUNK
 FIRST_BANKS = 5
 SECOND_BANKS = 3
-SCALE_ROW0 = 96
+STORE_ROWS = 2
+SCALE_ROW0 = P - PASSES * BLOCKS
 LISTS = ("size", "pred", "col")
 W3_COL = len(LISTS) * S
 W2_COL = W3_COL + H
 PLANE = W2_COL + H
-AFTER_W1 = ("words_size10", "words_pred10")
-REUSED = {"words_pred11": "w1_raw1", "words_col10": "pred2", "words_col11": "pred3"}
-POOL_CHUNKS = 4
 
 
 def tile_list_sketch_cardinality_kernel(
@@ -47,13 +47,14 @@ def tile_list_sketch_cardinality_kernel(
         tiles = {}
         opened = []
 
-        def held(name, shape, dtype, tag=None):
-            tiles[name] = keep.tile(shape, dtype, name=name, tag=tag or name, align_bytes=64)
+        def held(name, shape, dtype, reuse=None):
+            tiles[name] = keep.tile(shape, dtype, name=name, tag=reuse or name, align_bytes=64)
             return tiles[name]
 
         def placed(name, shape, dtype, offset):
             tiles[name] = shared.tile(shape, dtype, name=name, tag=name, align_bytes=64, offset=offset)
             return tiles[name]
+
 
         def load_list(name, src):
             nc.sync.dma_start(held("list_" + name, [P, S // 16], U16)[:], src)
@@ -67,20 +68,12 @@ def tile_list_sketch_cardinality_kernel(
             raw = held(name, [P, H // 4], I32)
             nc.sync.dma_start(raw[SCALE_ROW0:P, :], src.bitcast(I32).rearrange("a q c -> (a q) c"))
 
-        def stage_weight_scales(name, col0):
-            nc.gpsimd.tensor_copy(
-                tiles["staged"][SCALE_ROW0:P, col0 : col0 + H // 4].rearrange("p (t g i) -> p t g i", t=SLOTS, i=2),
-                tiles[name][SCALE_ROW0:P, :].rearrange("p (g t i) -> p t g i", t=SLOTS, i=2),
-            )
-
-        def load_w2():
-            nc.sync.dma_start(held("w2_raw", [P, PASSES, H // 2], I32)[:], w2_words.rearrange("a p c -> p a c").bitcast(I32))
-
-        def load_w3():
-            nc.sync.dma_start(held("w3_raw", [P, PASSES, H], I32)[:], w3_words.rearrange("a p c i -> p a (c i)").bitcast(I32))
+        def load_weight_words(name, words, src):
+            nc.sync.dma_start(held(name, [P, PASSES, words], I32)[:], src.bitcast(I32))
 
         def load_table(a):
-            nc.sync.dma_start(held("word_table%d" % a, [P, T], I32)[:], tab_words[a].rearrange("p t i -> p (t i)").bitcast(I32))
+            src = tab_words[a].rearrange("p t i -> p (t i)").bitcast(I32)
+            nc.sync.dma_start(held("word_table%d" % a, [P, T], I32)[:], src)
 
         def load_w1(a):
             rows = w1[512 * a : 512 * (a + 1), :].rearrange("(p s) c -> p s c", s=SLOTS)
@@ -88,7 +81,7 @@ def tile_list_sketch_cardinality_kernel(
 
         def load_w4():
             raw = held("w4_raw", [P, SLOTS, N], F32)
-            rows = w4.rearrange("(g t i) n -> t g i n", t=SLOTS, i=8)
+            rows = w4.rearrange("(g t i) n -> t g i n", t=SLOTS, i=RUN)
             for t in range(SLOTS):
                 nc.sync.dma_start(raw[:, t, :], rows[t])
 
@@ -96,56 +89,55 @@ def tile_list_sketch_cardinality_kernel(
             with nc.allow_non_contiguous_dma(reason="one bias value a partition"):
                 nc.sync.dma_start(held("bias", [P, N // P], F32)[:], b.rearrange("(t p) -> p t", p=P))
 
-        def permute(engine, name, raw, run, rows):
-            dst = held(name, [P, SLOTS, rows, 16 * run], I32)
-            engine.tensor_copy(
-                dst[:].rearrange("p t a (g i) -> p t (a g) i", i=run),
-                tiles[raw][:].rearrange("p a (g t i) -> p t (a g) i", t=SLOTS, i=run),
-            )
-
-        def gather_scales():
-            window = tiles["scale_table"][:].bitcast(U8)
-            picked = held("picked_scales", [P, len(LISTS) * S], U8)
-            for u, name in enumerate(LISTS):
-                nc.vector.tensor_copy(picked[:, u * S : (u + 1) * S], window.indirect(tiles["list_" + name][:]))
-            staged = placed("staged", [P, PLANE // 4], I32, 0)
-            nc.vector.tensor_copy(staged[SCALE_ROW0:P, 0 : W3_COL // 4], picked[:].bitcast(I32)[SCALE_ROW0:P, :])
 
         def clear_planes():
             for a in range(PASSES):
                 nc.gpsimd.memset(held("plane%d" % a, [P, PLANE // 4], I32)[:], 0)
 
-        def place_planes(a):
-            src = tiles["staged"]
-            for r in range(4):
-                row = SCALE_ROW0 + 16 * a
-                nc.scalar.dma_start(tiles["plane%d" % a][r:P:32, :], src[row + r : row + 16 : 4, :])
+        def gather_scales():
+            window = tiles["scale_table"][:].bitcast(U8)
+            picked = held("picked_scales", [P, W3_COL], U8)
+            for u, name in enumerate(LISTS):
+                nc.vector.tensor_copy(picked[:, u * S : (u + 1) * S], window.indirect(tiles["list_" + name][:]))
+            staged = placed("staged", [P, PLANE // 4], I32, 0)
+            nc.vector.tensor_copy(staged[SCALE_ROW0:P, 0 : W3_COL // 4], picked[:].bitcast(I32)[SCALE_ROW0:P, :])
 
-        def gather_words(name, half, a):
+        def stage_weight_scales(name, col0):
+            words = RUN // 4
+            dst = tiles["staged"][SCALE_ROW0:P, col0 // 4 : (col0 + H) // 4]
+            nc.gpsimd.tensor_copy(
+                dst.rearrange("p (t g i) -> p t g i", t=SLOTS, i=words),
+                tiles[name][SCALE_ROW0:P, :].rearrange("p (g t i) -> p t g i", t=SLOTS, i=words),
+            )
+
+        def place_plane(a):
+            row0 = SCALE_ROW0 + BLOCKS * a
+            for r in range(4):
+                nc.scalar.dma_start(tiles["plane%d" % a][r:P:32, :], tiles["staged"][row0 + r : row0 + BLOCKS : 4, :])
+
+        def plane(a, col0):
+            return tiles["plane%d" % a][:].bitcast(U8)[:, col0 : col0 + P]
+
+
+        def reorder_words(name, raw, words):
+            dst = held(name, [P, SLOTS, PASSES, BLOCKS * words], I32)
+            nc.gpsimd.tensor_copy(
+                dst[:].rearrange("p t a (g i) -> p t (a g) i", i=words),
+                tiles[raw][:].rearrange("p a (g t i) -> p t (a g) i", t=SLOTS, i=words),
+            )
+
+        def gather_words(name, half, a, reuse=None, offset=None):
             label = "words_%s%d%d" % (name, half, a)
-            if label in AFTER_W1:
-                dst = placed(label, [P, HALF], U32, 4 * HALF * AFTER_W1.index(label))
+            if offset is None:
+                dst = held(label, [P, HALF], U32, reuse)
             else:
-                dst = held(label, [P, HALF], U32, tag=REUSED.get(label))
+                dst = placed(label, [P, HALF], U32, offset)
             cols = slice(half * HALF // 16, (half + 1) * HALF // 16)
             window = tiles["word_table%d" % a][:].bitcast(U32)
             nc.vector.tensor_copy(dst[:], window.indirect(tiles["list_" + name][:, cols]))
 
         def pool_round(dst, src):
             nc.gpsimd.tensor_scalar(dst, src, 1.0, 0.0, MULT, ADD)
-
-        def group_w1(engine_copy, a):
-            grouped = held("w1_grouped%d" % a, [P, SLOTS, 16, 8, SLOTS], BF16)
-            src = tiles["w1_raw%d" % a][:].rearrange("p s (g t i) -> p t g i s", t=SLOTS, i=8)
-            for t in range(SLOTS):
-                copy = nc.scalar.copy if a == 1 and t < 2 else engine_copy
-                copy(grouped[:, t], src[:, t])
-
-        def group_w4(engine_copy):
-            grouped = held("w4_grouped", [P, N, SLOTS], BF16)
-            src = tiles["w4_raw"][:].rearrange("p t n -> p n t")
-            for n0 in range(0, N, P):
-                engine_copy(grouped[:, n0 : n0 + P, :], src[:, n0 : n0 + P, :])
 
         def quantize(name, grouped_flat):
             width = grouped_flat.shape[1] // SLOTS
@@ -154,14 +146,18 @@ def tile_list_sketch_cardinality_kernel(
             nc.vector.quantize_mx(out=codes[:].bitcast(FP8X4), scales=scales[:], in_=grouped_flat)
             return codes, scales
 
-        def quantize_w1(a):
-            quantize("w1_%d" % a, tiles["w1_grouped%d" % a][:].rearrange("p t g i s -> p (t g i s)"))
+        def prepare_w1(a, copies):
+            grouped = held("w1_grouped%d" % a, [P, SLOTS, BLOCKS, RUN, SLOTS], BF16)
+            src = tiles["w1_raw%d" % a][:].rearrange("p s (g t i) -> p t g i s", t=SLOTS, i=RUN)
+            for t, copy in enumerate(copies):
+                copy(grouped[:, t], src[:, t])
+            quantize("w1_%d" % a, grouped[:].rearrange("p t g i s -> p (t g i s)"))
 
-        def quantize_w4():
-            quantize("w4", tiles["w4_grouped"][:].rearrange("p n t -> p (n t)"))
-
-        def plane(a, col0):
-            return tiles["plane%d" % a][:].bitcast(U8)[:, col0 : col0 + P]
+        def round_w4():
+            grouped = held("w4_grouped", [P, N, SLOTS], BF16)
+            src = tiles["w4_raw"][:].rearrange("p t n -> p n t")
+            for n0 in range(0, N, P):
+                nc.scalar.copy(grouped[:, n0 : n0 + P, :], src[:, n0 : n0 + P, :])
 
         def stationary(name, a, t):
             if name == "size":
@@ -171,11 +167,11 @@ def tile_list_sketch_cardinality_kernel(
             cols = slice(t * P, (t + 1) * P)
             return tiles["w1_%d_codes" % a][:, cols].bitcast(FP8X4), tiles["w1_%d_scales" % a][:, cols]
 
+
         def product(name, chunk):
             bank = psum.tile([P, SLOTS, CHUNK], F32, name="first", tag="first%d" % (len(opened) % FIRST_BANKS))
             opened.append(name)
             half, c0 = divmod(chunk * CHUNK, HALF)
-            j0 = LISTS.index(name) * S + chunk * CHUNK
             for a in range(PASSES):
                 for t in range(SLOTS):
                     codes, scale = stationary(name, a, t)
@@ -184,7 +180,7 @@ def tile_list_sketch_cardinality_kernel(
                         lhsT=codes,
                         lhsT_scale=scale,
                         rhs=tiles["words_%s%d%d" % (name, half, a)][:, c0 : c0 + CHUNK].bitcast(FP8X4),
-                        rhs_scale=plane(a, j0),
+                        rhs_scale=plane(a, LISTS.index(name) * S + chunk * CHUNK),
                         start=(a == 0 and t == 0),
                         stop=(a == PASSES - 1 and t == SLOTS - 1),
                     )
@@ -197,15 +193,16 @@ def tile_list_sketch_cardinality_kernel(
             nc.scalar.copy(held("pred%d" % chunk, [P, CHUNK, SLOTS], F32)[:], product("pred", chunk))
 
         def smaller(chunk, col):
-            dst = held("smaller%d" % chunk, [P, CHUNK, SLOTS], F32, tag=None)
+            dst = held("smaller%d" % chunk, [P, CHUNK, SLOTS], F32)
             nc.vector.tensor_tensor(dst[:], col, tiles["pred%d" % chunk][:], MIN)
 
-        def times(chunk):
-            engine = nc.gpsimd if chunk < POOL_CHUNKS else nc.vector
+        def times(engine, chunk):
             pair = "h%d" % (chunk // 2)
-            if pair not in tiles:
+            if chunk % 2 == 0:
                 held(pair, [P, 2, CHUNK, SLOTS], BF16)
-            engine.tensor_tensor(tiles[pair][:, chunk % 2], tiles["smaller%d" % chunk][:], tiles["factor%d" % chunk][:], MULT)
+            dst = tiles[pair][:, chunk % 2]
+            engine.tensor_tensor(dst, tiles["smaller%d" % chunk][:], tiles["factor%d" % chunk][:], MULT)
+
 
         out_view = out.rearrange("(t p) j -> p t j", p=P)
 
@@ -214,12 +211,12 @@ def tile_list_sketch_cardinality_kernel(
             j0 = chunk * CHUNK
             h_part = tiles["h%d" % (chunk // 2)][:, chunk % 2 : chunk % 2 + count]
             codes, scales = quantize("hq%d" % chunk, h_part.rearrange("p u j t -> p (u j t)"))
-            group = 2
-            for n0 in range(0, N // P, group):
+            group = SLOTS * CHUNK // width
+            for t0 in range(0, N // P, group):
                 bank = psum.tile([P, group, width], F32, name="second", bufs=SECOND_BANKS)
-                result = held("result%d_%d" % (chunk, n0), [P, group, width], F32)
+                result = held("result%d_%d" % (chunk, t0), [P, group, width], F32)
                 for u in range(group):
-                    cols = slice((n0 + u) * P, (n0 + u + 1) * P)
+                    cols = slice((t0 + u) * P, (t0 + u + 1) * P)
                     nc.tensor.matmul_mx(
                         out=bank[:, u, :],
                         lhsT=tiles["w4_codes"][:, cols].bitcast(FP8X4),
@@ -229,9 +226,13 @@ def tile_list_sketch_cardinality_kernel(
                         start=True,
                         stop=True,
                     )
-                for u in range(group):
-                    nc.scalar.activation(result[:, u, :], bank[:, u, :], EXP, bias=tiles["bias"][:, n0 + u : n0 + u + 1])
-                nc.sync.dma_start(out_view[:, n0 : n0 + group, j0 : j0 + width], result[:])
+                for u0 in range(0, group, STORE_ROWS):
+                    rows = slice(u0, u0 + STORE_ROWS)
+                    for u in range(rows.start, rows.stop):
+                        bias = tiles["bias"][:, t0 + u : t0 + u + 1]
+                        nc.scalar.activation(result[:, u, :], bank[:, u, :], EXP, bias=bias)
+                    dst = out_view[:, t0 + rows.start : t0 + rows.stop, j0 : j0 + width]
+                    nc.sync.dma_start(dst, result[:, rows, :])
 
         load_table_scales()
         load_list("size", offs3)
@@ -240,17 +241,17 @@ def tile_list_sketch_cardinality_kernel(
         clear_planes()
         load_weight_scales("w3_scale_raw", w3_scales)
         load_weight_scales("w2_scale_raw", w2_scales)
-        load_w3()
-        load_w2()
+        load_weight_words("w3_raw", H, w3_words.rearrange("a p c i -> p a (c i)"))
+        load_weight_words("w2_raw", H // 2, w2_words.rearrange("a p c -> p a c"))
         load_table(0)
         load_table(1)
         gather_scales()
-        stage_weight_scales("w3_scale_raw", W3_COL // 4)
-        stage_weight_scales("w2_scale_raw", W2_COL // 4)
-        place_planes(0)
-        place_planes(1)
-        permute(nc.vector, "w3_codes", "w3_raw", 8, PASSES)
-        permute(nc.vector, "w2_codes", "w2_raw", 4, PASSES)
+        stage_weight_scales("w3_scale_raw", W3_COL)
+        stage_weight_scales("w2_scale_raw", W2_COL)
+        place_plane(0)
+        place_plane(1)
+        reorder_words("w3_codes", "w3_raw", RUN)
+        reorder_words("w2_codes", "w2_raw", RUN // 2)
         load_w1(0)
         load_w1(1)
         load_w4()
@@ -260,34 +261,33 @@ def tile_list_sketch_cardinality_kernel(
         for name in LISTS:
             for a in range(PASSES):
                 gather_words(name, 0, a)
-        for a in range(PASSES):
-            gather_words("size", 1, a)
-        gather_words("pred", 1, 0)
-        for a in range(PASSES):
-            group_w1(pool_round, a)
-            quantize_w1(a)
-        gather_words("pred", 1, 1)
+        gather_words("size", 1, 0, offset=0)
+        gather_words("size", 1, 1)
+        gather_words("pred", 1, 0, offset=4 * HALF)
+        prepare_w1(0, [pool_round] * SLOTS)
+        prepare_w1(1, [nc.scalar.copy, nc.scalar.copy, pool_round, nc.vector.tensor_copy])
+        gather_words("pred", 1, 1, reuse="w1_raw1")
         for chunk in first:
             size(chunk)
         for chunk in first:
             pred(chunk)
         for chunk in second:
             size(chunk)
-        group_w4(nc.scalar.copy)
+        round_w4()
         for chunk in first:
             smaller(chunk, product("col", chunk))
-            times(chunk)
+            times(nc.gpsimd, chunk)
         for chunk in second:
             pred(chunk)
         for a in range(PASSES):
-            gather_words("col", 1, a)
+            gather_words("col", 1, a, reuse="pred%d" % (CHUNKS - PASSES + a))
         cols = [product("col", chunk) for chunk in second]
-        quantize_w4()
+        quantize("w4", tiles["w4_grouped"][:].rearrange("p n t -> p (n t)"))
         head(0, 2)
         head(2, 2)
-        smaller(CHUNKS, cols[0])
+        smaller(second.start, cols[0])
         for chunk in second:
             if chunk + 1 in second:
-                smaller(chunk + 1, cols[chunk + 1 - CHUNKS])
-            times(chunk)
+                smaller(chunk + 1, cols[chunk + 1 - second.start])
+            times(nc.vector, chunk)
             head(chunk, 1)

@@ -22,6 +22,7 @@ P = 128
 PASSES = K // 512
 SLOTS = 4
 RUN = 8
+LINE = 4
 BLOCKS = 16
 HALF = S // 2
 CHUNK = 128
@@ -150,14 +151,20 @@ def tile_list_sketch_cardinality_kernel(
             grouped = held("w1_grouped%d" % a, [P, SLOTS, BLOCKS, RUN, SLOTS], BF16)
             src = tiles["w1_raw%d" % a][:].rearrange("p s (g t i) -> p t g i s", t=SLOTS, i=RUN)
             for t, copy in enumerate(copies):
-                copy(grouped[:, t], src[:, t])
+                if copy == pool_round:
+                    copy(grouped[:, t], src[:, t])
+                else:
+                    by_line = "p g (u i) s -> p g u s i"
+                    copy(grouped[:, t].rearrange(by_line, i=LINE), src[:, t].rearrange(by_line, i=LINE))
             quantize("w1_%d" % a, grouped[:].rearrange("p t g i s -> p (t g i s)"))
 
         def round_w4():
             grouped = held("w4_grouped", [P, N, SLOTS], BF16)
             src = tiles["w4_raw"][:].rearrange("p t n -> p n t")
             for n0 in range(0, N, P):
-                nc.scalar.copy(grouped[:, n0 : n0 + P, :], src[:, n0 : n0 + P, :])
+                by_line = "p (u i) t -> p u t i"
+                cols = slice(n0, n0 + P)
+                nc.scalar.copy(grouped[:, cols].rearrange(by_line, i=LINE), src[:, cols].rearrange(by_line, i=LINE))
 
         def stationary(name, a, t):
             if name == "size":

@@ -272,7 +272,7 @@ def tile_list_sketch_cardinality_kernel(
         gather_words("size", 1, 1)
         gather_words("pred", 1, 0, offset=4 * HALF)
         prepare_w1(0, [pool_round] * SLOTS)
-        prepare_w1(1, [nc.scalar.copy, nc.scalar.copy, pool_round, nc.vector.tensor_copy])
+        prepare_w1(1, [nc.scalar.copy, nc.scalar.copy, nc.scalar.copy, pool_round])
         gather_words("pred", 1, 1, reuse="w1_raw1")
         for chunk in first:
             size(chunk)
@@ -292,9 +292,15 @@ def tile_list_sketch_cardinality_kernel(
         quantize("w4", tiles["w4_grouped"][:].rearrange("p n t -> p (n t)"))
         head(0, 2)
         head(2, 2)
-        smaller(second.start, cols[0])
-        for chunk in second:
-            if chunk + 1 in second:
-                smaller(chunk + 1, cols[chunk + 1 - second.start])
-            times(nc.vector, chunk)
-            head(chunk, 1)
+        smaller(4, cols[0])
+        times(nc.gpsimd, 4)
+        smaller(5, cols[1])
+        smaller(6, cols[2])
+        times(nc.vector, 5)
+        smaller(7, cols[3])
+        head(4, 1)
+        times(nc.vector, 6)
+        head(5, 1)
+        times(nc.vector, 7)
+        head(6, 1)
+        head(7, 1)

@@ -1,3 +1,4 @@
+import math
 from contextlib import ExitStack
 
 import concourse.mybir as mybir
@@ -11,6 +12,7 @@ I32 = mybir.dt.int32
 U32 = mybir.dt.uint32
 U16 = mybir.dt.uint16
 U8 = mybir.dt.uint8
+NBYTES = {F32: 4, BF16: 2, I32: 4, U32: 4, U8: 1}
 FP8X4 = mybir.dt.float8_e4m3fn_x4
 FP4X4 = mybir.dt.float4_e2m1fn_x4
 EXP = mybir.ActivationFunctionType.Exp
@@ -26,15 +28,12 @@ LINE = 4
 BLOCKS = 16
 HALF = S // 2
 CHUNK = 128
-CHUNKS = HALF // CHUNK
-FIRST_BANKS = 5
-SECOND_BANKS = 3
+PAIR = 2 * CHUNK
+KIB = 1024
 STORE_ROWS = 2
 SCALE_ROW0 = P - PASSES * BLOCKS
-LISTS = ("size", "pred", "col")
-W3_COL = len(LISTS) * S
-W2_COL = W3_COL + H
-PLANE = W2_COL + H
+LISTS = ("pred", "size", "col")
+PICKED = len(LISTS) * S
 
 
 def tile_list_sketch_cardinality_kernel(
@@ -42,194 +41,230 @@ def tile_list_sketch_cardinality_kernel(
 ):
     nc = tc.nc
     with ExitStack() as ctx:
-        keep = ctx.enter_context(tc.tile_pool(name="keep", bufs=1))
-        shared = ctx.enter_context(tc.tile_pool(name="shared", bufs=1))
+        lists = ctx.enter_context(tc.tile_pool(name="lists", bufs=1))
+        work = ctx.enter_context(tc.tile_pool(name="work", bufs=1))
         psum = ctx.enter_context(tc.psum_pool(name="psum", bufs=1))
         tiles = {}
-        opened = []
+        start = {}
+        ends = [0]
 
-        def held(name, shape, dtype, reuse=None):
-            tiles[name] = keep.tile(shape, dtype, name=name, tag=reuse or name, align_bytes=64)
+        def held(name, shape, dtype, over=None, at=0, below=0, above=0):
+            if over is None:
+                start[name] = ends[-1] + below
+                ends.append(start[name] + math.prod(shape[1:]) * NBYTES[dtype] + above)
+                ends[-1] = (ends[-1] + 63) // 64 * 64
+            else:
+                start[name] = start[over] + at
+            tiles[name] = work.tile(shape, dtype, name=name, tag=name, align_bytes=64, offset=start[name])
             return tiles[name]
 
-        def placed(name, shape, dtype, offset):
-            tiles[name] = shared.tile(shape, dtype, name=name, tag=name, align_bytes=64, offset=offset)
-            return tiles[name]
+        def bank(number, role):
+            return psum.tile([P, SLOTS * CHUNK], F32, name=role, tag="bank%d" % number)
 
 
         def load_list(name, src):
-            nc.sync.dma_start(held("list_" + name, [P, S // 16], U16)[:], src)
+            tiles["list_" + name] = lists.tile([P, S // 16], U16, name="list_" + name, tag="list_" + name)
+            nc.sync.dma_start(tiles["list_" + name][:], src)
 
         def load_table_scales():
-            window = held("scale_table", [P, T // 4], I32)
-            nc.sync.dma_start(window[SCALE_ROW0:P, :], tab_scales.bitcast(I32).rearrange("a q c -> (a q) c"))
-            nc.vector.memset(window[0:SCALE_ROW0, :], 0)
+            window = held("scale_table", [P, T // 4], I32, below=8 * KIB)
+            nc.gpsimd.memset(window[0:SCALE_ROW0, :], 0)
+            rows = tab_scales.bitcast(I32).rearrange("a (q r) c -> r q a c", r=4)
+            for r in range(4):
+                nc.sync.dma_start(window[SCALE_ROW0 + r : P : 4, :], rows[r])
+
+        def clear_weight_scales(name, over=None, at=0):
+            nc.gpsimd.memset(held(name, [P, PASSES, H // 4], I32, over, at)[:], 0)
 
         def load_weight_scales(name, src):
-            raw = held(name, [P, H // 4], I32)
-            nc.sync.dma_start(raw[SCALE_ROW0:P, :], src.bitcast(I32).rearrange("a q c -> (a q) c"))
+            raw = tiles[name]
+            rows = src.bitcast(I32).rearrange("a (q r) c -> q r a c", r=4)
+            for q in range(4):
+                nc.sync.dma_start(raw[32 * q : 32 * q + 4], rows[q])
 
-        def load_weight_words(name, words, src):
-            nc.sync.dma_start(held(name, [P, PASSES, words], I32)[:], src.bitcast(I32))
+        def load_weight_words(name, words, src, over=None, at=0):
+            nc.sync.dma_start(held(name, [P, PASSES, words], I32, over, at)[:], src.bitcast(I32))
 
         def load_table(a):
             src = tab_words[a].rearrange("p t i -> p (t i)").bitcast(I32)
             nc.sync.dma_start(held("word_table%d" % a, [P, T], I32)[:], src)
 
-        def load_w1(a):
+        def load_w1(a, over, at):
             rows = w1[512 * a : 512 * (a + 1), :].rearrange("(p s) c -> p s c", s=SLOTS)
-            nc.sync.dma_start(held("w1_raw%d" % a, [P, SLOTS, H], F32)[:], rows)
+            nc.sync.dma_start(held("w1_raw%d" % a, [P, SLOTS, H], F32, over, at)[:], rows)
 
         def load_w4():
-            raw = held("w4_raw", [P, SLOTS, N], F32)
+            raw = held("w4_raw", [P, SLOTS, N], F32, "picked_scales", PICKED - 64)
             rows = w4.rearrange("(g t i) n -> t g i n", t=SLOTS, i=RUN)
             for t in range(SLOTS):
                 nc.sync.dma_start(raw[:, t, :], rows[t])
 
         def load_bias():
             with nc.allow_non_contiguous_dma(reason="one bias value a partition"):
-                nc.sync.dma_start(held("bias", [P, N // P], F32)[:], b.rearrange("(t p) -> p t", p=P))
+                nc.sync.dma_start(held("bias", [P, N // P], F32, "scale_table", 2 * KIB)[:], b.rearrange("(t p) -> p t", p=P))
 
 
         def clear_planes():
-            for a in range(PASSES):
-                nc.gpsimd.memset(held("plane%d" % a, [P, PLANE // 4], I32)[:], 0)
+            nc.gpsimd.memset(held("planes", [P, PASSES * PICKED // 4], I32)[:], 0)
 
         def gather_scales():
             window = tiles["scale_table"][:].bitcast(U8)
-            picked = held("picked_scales", [P, W3_COL], U8)
+            picked = held("picked_scales", [P, PICKED], U8, below=12 * KIB, above=8 * KIB)
             for u, name in enumerate(LISTS):
                 nc.vector.tensor_copy(picked[:, u * S : (u + 1) * S], window.indirect(tiles["list_" + name][:]))
-            staged = placed("staged", [P, PLANE // 4], I32, 0)
-            nc.vector.tensor_copy(staged[SCALE_ROW0:P, 0 : W3_COL // 4], picked[:].bitcast(I32)[SCALE_ROW0:P, :])
 
-        def stage_weight_scales(name, col0):
+        def reorder_scales(copy, name, raw):
             words = RUN // 4
-            dst = tiles["staged"][SCALE_ROW0:P, col0 // 4 : (col0 + H) // 4]
-            nc.gpsimd.tensor_copy(
-                dst.rearrange("p (t g i) -> p t g i", t=SLOTS, i=words),
-                tiles[name][SCALE_ROW0:P, :].rearrange("p (g t i) -> p t g i", t=SLOTS, i=words),
+            dst = held(name, [P, PASSES, H // 4], U32)
+            copy(
+                dst[:].rearrange("p a (t g i) -> p a t g i", t=SLOTS, i=words),
+                tiles[raw][:].bitcast(U32).rearrange("p a (g t i) -> p a t g i", t=SLOTS, i=words),
             )
 
-        def place_plane(a):
-            row0 = SCALE_ROW0 + BLOCKS * a
+        def place_planes():
+            picked = tiles["picked_scales"][:].bitcast(I32)
             for r in range(4):
-                nc.scalar.dma_start(tiles["plane%d" % a][r:P:32, :], tiles["staged"][row0 + r : row0 + BLOCKS : 4, :])
+                dst = tiles["planes"][r:P:32, :].rearrange("p (a c) -> p a c", a=PASSES)
+                nc.sync.dma_start(dst, picked[SCALE_ROW0 + r : P : 4, :])
 
-        def plane(a, col0):
-            return tiles["plane%d" % a][:].bitcast(U8)[:, col0 : col0 + P]
+        def plane(a, col0, width):
+            return tiles["planes"][:].bitcast(U8)[:, a * PICKED + col0 : a * PICKED + col0 + width]
+
+        def weight_plane(name, a, t):
+            return tiles[name][:, a].bitcast(U8)[:, t * P : (t + 1) * P]
 
 
-        def reorder_words(name, raw, words):
-            dst = held(name, [P, SLOTS, PASSES, BLOCKS * words], I32)
-            nc.gpsimd.tensor_copy(
+        def reorder_words(copy, name, raw, words):
+            dst = held(name, [P, SLOTS, PASSES, BLOCKS * words], U32)
+            copy(
                 dst[:].rearrange("p t a (g i) -> p t (a g) i", i=words),
-                tiles[raw][:].rearrange("p a (g t i) -> p t (a g) i", t=SLOTS, i=words),
+                tiles[raw][:].bitcast(U32).rearrange("p a (g t i) -> p t (a g) i", t=SLOTS, i=words),
             )
 
-        def gather_words(name, half, a, reuse=None, offset=None):
-            label = "words_%s%d%d" % (name, half, a)
-            if offset is None:
-                dst = held(label, [P, HALF], U32, reuse)
-            else:
-                dst = placed(label, [P, HALF], U32, offset)
-            cols = slice(half * HALF // 16, (half + 1) * HALF // 16)
+        def gather(dst, name, j0, count, a):
             window = tiles["word_table%d" % a][:].bitcast(U32)
-            nc.vector.tensor_copy(dst[:], window.indirect(tiles["list_" + name][:, cols]))
+            nc.vector.tensor_copy(dst, window.indirect(tiles["list_" + name][:, j0 // 16 : (j0 + count) // 16]))
+
+        def gather_half(name, half, a, over=None, at=0, spare=0):
+            gather(held("words_%s%d%d" % (name, half, a), [P, HALF], U32, over, at, spare, spare)[:], name, half * HALF, HALF, a)
+
+        def gather_col(pair, over, at=0):
+            dst = held("words_col%d" % pair, [P, PASSES, PAIR], U32, over, at)
+            for a in range(PASSES):
+                gather(dst[:, a, :], "col", pair * PAIR, PAIR, a)
+
+        def words(name, j0, width, a):
+            if name == "col":
+                return tiles["words_col%d" % (j0 // PAIR)][:, a, j0 % PAIR : j0 % PAIR + width]
+            return tiles["words_%s%d%d" % (name, j0 // HALF, a)][:, j0 % HALF : j0 % HALF + width]
 
         def pool_round(dst, src):
             nc.gpsimd.tensor_scalar(dst, src, 1.0, 0.0, MULT, ADD)
 
-        def quantize(name, grouped_flat):
+        def scalar_round(dst, src):
+            by_line = "p g (u i) s -> p g u s i"
+            nc.scalar.copy(dst.rearrange(by_line, i=LINE), src.rearrange(by_line, i=LINE))
+
+        def quantize(name, grouped_flat, over=None):
             width = grouped_flat.shape[1] // SLOTS
-            codes = held(name + "_codes", [P, width], U32)
+            codes = held(name + "_codes", [P, width], U32, over)
             scales = held(name + "_scales", [P, width], U8)
             nc.vector.quantize_mx(out=codes[:].bitcast(FP8X4), scales=scales[:], in_=grouped_flat)
             return codes, scales
 
-        def prepare_w1(a, copies):
-            grouped = held("w1_grouped%d" % a, [P, SLOTS, BLOCKS, RUN, SLOTS], BF16)
+        def round_w1(a, copies, above=0):
+            grouped = held("w1_grouped%d" % a, [P, SLOTS, BLOCKS, RUN, SLOTS], BF16, above=above)
             src = tiles["w1_raw%d" % a][:].rearrange("p s (g t i) -> p t g i s", t=SLOTS, i=RUN)
             for t, copy in enumerate(copies):
-                if copy == pool_round:
-                    copy(grouped[:, t], src[:, t])
-                else:
-                    by_line = "p g (u i) s -> p g u s i"
-                    copy(grouped[:, t].rearrange(by_line, i=LINE), src[:, t].rearrange(by_line, i=LINE))
-            quantize("w1_%d" % a, grouped[:].rearrange("p t g i s -> p (t g i s)"))
+                copy(grouped[:, t], src[:, t])
 
-        def round_w4():
-            grouped = held("w4_grouped", [P, N, SLOTS], BF16)
-            src = tiles["w4_raw"][:].rearrange("p t n -> p n t")
-            for n0 in range(0, N, P):
-                by_line = "p (u i) t -> p u t i"
-                cols = slice(n0, n0 + P)
-                nc.scalar.copy(grouped[:, cols].rearrange(by_line, i=LINE), src[:, cols].rearrange(by_line, i=LINE))
+        def quantize_w1(a):
+            quantize("w1_%d" % a, tiles["w1_grouped%d" % a][:].rearrange("p t g i s -> p (t g i s)"))
+
+        def round_w4(copies):
+            grouped = held("w4_grouped", [P, N // P, BLOCKS, RUN, SLOTS], BF16, "w1_grouped1", 2 * KIB)
+            src = tiles["w4_raw"][:].rearrange("p s (t g i) -> p t g i s", t=N // P, i=RUN)
+            for t, copy in enumerate(copies):
+                copy(grouped[:, t], src[:, t])
 
         def stationary(name, a, t):
             if name == "size":
-                return tiles["w3_codes"][:, t, a, :].bitcast(FP8X4), plane(a, W3_COL + t * P)
+                return tiles["w3_codes"][:, t, a, :].bitcast(FP8X4), weight_plane("w3_planes", a, t)
             if name == "pred":
-                return tiles["w2_codes"][:, t, a, :].bitcast(U8).bitcast(FP4X4), plane(a, W2_COL + t * P)
+                return tiles["w2_codes"][:, t, a, :].bitcast(U8).bitcast(FP4X4), weight_plane("w2_planes", a, t)
             cols = slice(t * P, (t + 1) * P)
             return tiles["w1_%d_codes" % a][:, cols].bitcast(FP8X4), tiles["w1_%d_scales" % a][:, cols]
 
 
-        def product(name, chunk):
-            bank = psum.tile([P, SLOTS, CHUNK], F32, name="first", tag="first%d" % (len(opened) % FIRST_BANKS))
-            opened.append(name)
-            half, c0 = divmod(chunk * CHUNK, HALF)
+        def product(name, number, j0, slots):
+            width = SLOTS * CHUNK // len(slots)
+            sums = bank(number, name)[:].rearrange("p (t j) -> p t j", j=width)
             for a in range(PASSES):
-                for t in range(SLOTS):
+                for u, t in enumerate(slots):
                     codes, scale = stationary(name, a, t)
                     nc.tensor.matmul_mx(
-                        out=bank[:, t, :],
+                        out=sums[:, u, :],
                         lhsT=codes,
                         lhsT_scale=scale,
-                        rhs=tiles["words_%s%d%d" % (name, half, a)][:, c0 : c0 + CHUNK].bitcast(FP8X4),
-                        rhs_scale=plane(a, LISTS.index(name) * S + chunk * CHUNK),
-                        start=(a == 0 and t == 0),
-                        stop=(a == PASSES - 1 and t == SLOTS - 1),
+                        rhs=words(name, j0, width, a).bitcast(FP8X4),
+                        rhs_scale=plane(a, LISTS.index(name) * S + j0, width),
+                        start=(a == 0 and u == 0),
+                        stop=(a == PASSES - 1 and u == len(slots) - 1),
                     )
-            return bank[:].rearrange("p t j -> p j t")
+            return sums.rearrange("p t j -> p j t")
 
-        def size(chunk):
-            nc.scalar.activation(held("factor%d" % chunk, [P, CHUNK, SLOTS], F32)[:], product("size", chunk), EXP)
+        def size(pair, number, over, at):
+            dst = held("factor%d" % pair, [P, 2, CHUNK, SLOTS], F32, over, at)
+            for u in range(2):
+                sums = product("size", number + u, pair * PAIR + u * CHUNK, range(SLOTS))
+                nc.scalar.activation(dst[:, u], sums, EXP)
 
-        def pred(chunk):
-            nc.scalar.copy(held("pred%d" % chunk, [P, CHUNK, SLOTS], F32)[:], product("pred", chunk))
+        def pred(pair, number, over=None, at=0):
+            dst = held("pred%d" % pair, [P, 2, PAIR, 2], F32, over, at)
+            for u in range(2):
+                nc.scalar.copy(dst[:, u], product("pred", number + u, pair * PAIR, (2 * u, 2 * u + 1)))
 
-        def smaller(chunk, col):
-            dst = held("smaller%d" % chunk, [P, CHUNK, SLOTS], F32)
-            nc.vector.tensor_tensor(dst[:], col, tiles["pred%d" % chunk][:], MIN)
+        def col(chunk, number):
+            tiles["col%d" % chunk] = product("col", number, chunk * CHUNK, range(SLOTS))
+
+        def smaller(chunk, over=None, at=0):
+            if chunk % 2 == 0:
+                held("smaller%d" % (chunk // 2), [P, 2, CHUNK, 2, 2], F32, over, at)
+            dst = tiles["smaller%d" % (chunk // 2)][:, chunk % 2]
+            j0 = chunk % 2 * CHUNK
+            other = tiles["pred%d" % (chunk // 2)][:, :, j0 : j0 + CHUNK, :].rearrange("p u j s -> p j u s")
+            nc.vector.tensor_tensor(dst, tiles["col%d" % chunk].rearrange("p j (u s) -> p j u s", u=2), other, MIN)
 
         def times(engine, chunk):
-            pair = "h%d" % (chunk // 2)
-            if chunk % 2 == 0:
-                held(pair, [P, 2, CHUNK, SLOTS], BF16)
-            dst = tiles[pair][:, chunk % 2]
-            engine.tensor_tensor(dst, tiles["smaller%d" % chunk][:], tiles["factor%d" % chunk][:], MULT)
+            dst = tiles["h%d" % (chunk // 2)][:, chunk % 2]
+            src = tiles["smaller%d" % (chunk // 2)][:, chunk % 2].rearrange("p j u s -> p j (u s)")
+            engine.tensor_tensor(dst, src, tiles["factor%d" % (chunk // 2)][:, chunk % 2], MULT)
+
+        def h_pair(pair, over=None, at=0, below=0, above=0):
+            held("h%d" % pair, [P, 2, CHUNK, SLOTS], BF16, over, at, below, above)
 
 
         out_view = out.rearrange("(t p) j -> p t j", p=P)
 
-        def head(chunk, count):
+        def quantize_h(chunk, count, over=None):
+            h_part = tiles["h%d" % (chunk // 2)][:, chunk % 2 : chunk % 2 + count]
+            quantize("hq%d" % chunk, h_part.rearrange("p u j t -> p (u j t)"), over)
+
+        def head(chunk, count, number):
             width = count * CHUNK
             j0 = chunk * CHUNK
-            h_part = tiles["h%d" % (chunk // 2)][:, chunk % 2 : chunk % 2 + count]
-            codes, scales = quantize("hq%d" % chunk, h_part.rearrange("p u j t -> p (u j t)"))
             group = SLOTS * CHUNK // width
             for t0 in range(0, N // P, group):
-                bank = psum.tile([P, group, width], F32, name="second", bufs=SECOND_BANKS)
+                sums = bank(number + t0 // group, "last")[:].rearrange("p (u j) -> p u j", j=width)
                 result = held("result%d_%d" % (chunk, t0), [P, group, width], F32)
                 for u in range(group):
                     cols = slice((t0 + u) * P, (t0 + u + 1) * P)
                     nc.tensor.matmul_mx(
-                        out=bank[:, u, :],
+                        out=sums[:, u, :],
                         lhsT=tiles["w4_codes"][:, cols].bitcast(FP8X4),
                         lhsT_scale=tiles["w4_scales"][:, cols],
-                        rhs=codes[:].bitcast(FP8X4),
-                        rhs_scale=scales[:],
+                        rhs=tiles["hq%d_codes" % chunk][:].bitcast(FP8X4),
+                        rhs_scale=tiles["hq%d_scales" % chunk][:],
                         start=True,
                         stop=True,
                     )
@@ -237,70 +272,95 @@ def tile_list_sketch_cardinality_kernel(
                     rows = slice(u0, u0 + STORE_ROWS)
                     for u in range(rows.start, rows.stop):
                         bias = tiles["bias"][:, t0 + u : t0 + u + 1]
-                        nc.scalar.activation(result[:, u, :], bank[:, u, :], EXP, bias=bias)
+                        nc.scalar.activation(result[:, u, :], sums[:, u, :], EXP, bias=bias)
                     dst = out_view[:, t0 + rows.start : t0 + rows.stop, j0 : j0 + width]
                     nc.sync.dma_start(dst, result[:, rows, :])
 
+        clear_weight_scales("w2_scale_raw")
+        load_list("pred", offs2)
         load_table_scales()
         load_list("size", offs3)
-        load_list("pred", offs2)
         load_list("col", offs)
-        clear_planes()
-        load_weight_scales("w3_scale_raw", w3_scales)
-        load_weight_scales("w2_scale_raw", w2_scales)
-        load_weight_words("w3_raw", H, w3_words.rearrange("a p c i -> p a (c i)"))
-        load_weight_words("w2_raw", H // 2, w2_words.rearrange("a p c -> p a c"))
         load_table(0)
+        load_weight_words("w2_raw", H // 2, w2_words.rearrange("a p c -> p a c"))
+        load_weight_words("w3_raw", H, w3_words.rearrange("a p c i -> p a (c i)"))
+        load_weight_scales("w2_scale_raw", w2_scales)
         load_table(1)
+        clear_planes()
+        reorder_words(nc.scalar.copy, "w2_codes", "w2_raw", RUN // 2)
+        reorder_words(nc.scalar.copy, "w3_codes", "w3_raw", RUN)
+        reorder_scales(nc.scalar.copy, "w2_planes", "w2_scale_raw")
         gather_scales()
-        stage_weight_scales("w3_scale_raw", W3_COL)
-        stage_weight_scales("w2_scale_raw", W2_COL)
-        place_plane(0)
-        place_plane(1)
-        reorder_words("w3_codes", "w3_raw", RUN)
-        reorder_words("w2_codes", "w2_raw", RUN // 2)
-        load_w1(0)
-        load_w1(1)
+        place_planes()
+        load_w1(0, "scale_table", 64 - 8 * KIB)
+        clear_weight_scales("w3_scale_raw", "scale_table", KIB)
+        load_weight_scales("w3_scale_raw", w3_scales)
+        load_w1(1, "picked_scales", 64 - 8 * KIB)
         load_w4()
         load_bias()
 
-        first, second = range(CHUNKS), range(CHUNKS, 2 * CHUNKS)
-        for name in LISTS:
-            for a in range(PASSES):
-                gather_words(name, 0, a)
-        gather_words("size", 1, 0, offset=0)
-        gather_words("size", 1, 1)
-        gather_words("pred", 1, 0, offset=4 * HALF)
-        prepare_w1(0, [pool_round] * SLOTS)
-        prepare_w1(1, [nc.scalar.copy, nc.scalar.copy, nc.scalar.copy, pool_round])
-        gather_words("pred", 1, 1, reuse="w1_raw1")
-        for chunk in first:
-            size(chunk)
-        for chunk in first:
-            pred(chunk)
-        for chunk in second:
-            size(chunk)
-        round_w4()
-        for chunk in first:
-            smaller(chunk, product("col", chunk))
-            times(nc.gpsimd, chunk)
-        for chunk in second:
-            pred(chunk)
-        for a in range(PASSES):
-            gather_words("col", 1, a, reuse="pred%d" % (CHUNKS - PASSES + a))
-        cols = [product("col", chunk) for chunk in second]
-        quantize("w4", tiles["w4_grouped"][:].rearrange("p n t -> p (n t)"))
-        head(0, 2)
-        head(2, 2)
-        smaller(4, cols[0])
+        gather_half("pred", 0, 0)
+        gather_half("pred", 1, 0)
+        gather_half("size", 0, 0)
+        gather_half("pred", 0, 1)
+        gather_half("pred", 1, 1)
+        gather_half("size", 0, 1)
+        pred(0, 0)
+        pred(1, 2)
+        gather_half("size", 1, 1)
+        gather_half("size", 1, 0, over="words_pred01")
+        reorder_scales(nc.scalar.copy, "w3_planes", "w3_scale_raw")
+        pred(2, 4)
+        gather_col(0, over="words_pred11")
+        round_w1(0, [pool_round] * SLOTS)
+        round_w1(1, [scalar_round, scalar_round, scalar_round, pool_round], above=3 * KIB)
+        quantize_w1(0)
+        quantize_w1(1)
+        size(0, 0, "w1_raw1", 64 - 4 * KIB)
+        pred(3, 6, "w1_raw1", 64)
+        size(1, 2, "w1_raw1", 64 + 4 * KIB)
+        gather_col(1, over="w1_grouped1")
+        round_w4([scalar_round] * SLOTS)
+        col(0, 4)
+        col(1, 5)
+        h_pair(0, below=2 * KIB, above=5 * KIB)
+        smaller(0)
+        times(nc.gpsimd, 0)
+        smaller(1)
+        times(nc.gpsimd, 1)
+        col(2, 0)
+        col(3, 1)
+        gather_col(2, over="pred0")
+        smaller(2)
+        smaller(3)
+        size(2, 4, "w4_raw", 0)
+        size(3, 0, "w4_raw", 4 * KIB)
+        quantize("w4", tiles["w4_grouped"][:].rearrange("p t g i s -> p (t g i s)"), over="smaller0")
+        quantize_h(0, 2, over="w4_grouped")
+        col(4, 2)
+        col(5, 3)
+        head(0, 2, 6)
+        gather_col(3, over="h0", at=64 - 2 * KIB)
+        h_pair(1, over="h0", at=128)
+        times(nc.gpsimd, 2)
+        times(nc.gpsimd, 3)
+        smaller(4, over="w4_grouped", at=KIB)
+        smaller(5)
+        col(6, 4)
+        col(7, 5)
+        quantize_h(2, 2)
+        head(2, 2, 0)
+        h_pair(2, over="h1", at=-64)
         times(nc.gpsimd, 4)
-        smaller(5, cols[1])
-        smaller(6, cols[2])
+        smaller(6, over="h1", at=2 * KIB - 64)
+        smaller(7)
         times(nc.vector, 5)
-        smaller(7, cols[3])
-        head(4, 1)
+        quantize_h(4, 2)
+        head(4, 2, 2)
+        h_pair(3)
         times(nc.vector, 6)
-        head(5, 1)
         times(nc.vector, 7)
-        head(6, 1)
-        head(7, 1)
+        quantize_h(6, 1)
+        head(6, 1, 6)
+        quantize_h(7, 1)
+        head(7, 1, 7)

@@ -32,8 +32,8 @@ PAIR = 2 * CHUNK
 KIB = 1024
 STORE_ROWS = 2
 SCALE_ROW0 = P - PASSES * BLOCKS
-LISTS = ("pred", "size", "col")
-PICKED = len(LISTS) * S
+EARLY = ("pred",)
+LATE = ("size", "col")
 
 
 def tile_list_sketch_cardinality_kernel(
@@ -94,7 +94,7 @@ def tile_list_sketch_cardinality_kernel(
             nc.sync.dma_start(held("w1_raw%d" % a, [P, SLOTS, H], F32, over, at)[:], rows)
 
         def load_w4():
-            raw = held("w4_raw", [P, SLOTS, N], F32, "picked_scales", PICKED - 64)
+            raw = held("w4_raw", [P, SLOTS, N], F32, "picked_size", 2 * KIB - 64)
             rows = w4.rearrange("(g t i) n -> t g i n", t=SLOTS, i=RUN)
             for t in range(SLOTS):
                 nc.sync.dma_start(raw[:, t, :], rows[t])
@@ -104,13 +104,13 @@ def tile_list_sketch_cardinality_kernel(
                 nc.sync.dma_start(held("bias", [P, N // P], F32, "scale_table", 2 * KIB)[:], b.rearrange("(t p) -> p t", p=P))
 
 
-        def clear_planes():
-            nc.gpsimd.memset(held("planes", [P, PASSES * PICKED // 4], I32)[:], 0)
+        def clear_planes(names):
+            nc.gpsimd.memset(held("planes_" + names[0], [P, PASSES * len(names) * S // 4], I32)[:], 0)
 
-        def gather_scales():
+        def gather_scales(names, below=0, above=0):
             window = tiles["scale_table"][:].bitcast(U8)
-            picked = held("picked_scales", [P, PICKED], U8, below=12 * KIB, above=8 * KIB)
-            for u, name in enumerate(LISTS):
+            picked = held("picked_" + names[0], [P, len(names) * S], U8, below=below, above=above)
+            for u, name in enumerate(names):
                 nc.vector.tensor_copy(picked[:, u * S : (u + 1) * S], window.indirect(tiles["list_" + name][:]))
 
         def reorder_scales(copy, name, raw):
@@ -121,14 +121,16 @@ def tile_list_sketch_cardinality_kernel(
                 tiles[raw][:].bitcast(U32).rearrange("p a (g t i) -> p a t g i", t=SLOTS, i=words),
             )
 
-        def place_planes():
-            picked = tiles["picked_scales"][:].bitcast(I32)
+        def place_planes(names):
+            picked = tiles["picked_" + names[0]][:].bitcast(I32)
             for r in range(4):
-                dst = tiles["planes"][r:P:32, :].rearrange("p (a c) -> p a c", a=PASSES)
+                dst = tiles["planes_" + names[0]][r:P:32, :].rearrange("p (a c) -> p a c", a=PASSES)
                 nc.sync.dma_start(dst, picked[SCALE_ROW0 + r : P : 4, :])
 
-        def plane(a, col0, width):
-            return tiles["planes"][:].bitcast(U8)[:, a * PICKED + col0 : a * PICKED + col0 + width]
+        def plane(name, a, j0, width):
+            names = EARLY if name in EARLY else LATE
+            col0 = (a * len(names) + names.index(name)) * S + j0
+            return tiles["planes_" + names[0]][:].bitcast(U8)[:, col0 : col0 + width]
 
         def weight_plane(name, a, t):
             return tiles[name][:, a].bitcast(U8)[:, t * P : (t + 1) * P]
@@ -207,7 +209,7 @@ def tile_list_sketch_cardinality_kernel(
                         lhsT=codes,
                         lhsT_scale=scale,
                         rhs=words(name, j0, width, a).bitcast(FP8X4),
-                        rhs_scale=plane(a, LISTS.index(name) * S + j0, width),
+                        rhs_scale=plane(name, a, j0, width),
                         start=(a == 0 and u == 0),
                         stop=(a == PASSES - 1 and u == len(slots) - 1),
                     )
@@ -282,20 +284,23 @@ def tile_list_sketch_cardinality_kernel(
         load_list("size", offs3)
         load_list("col", offs)
         load_table(0)
+        load_weight_scales("w2_scale_raw", w2_scales)
         load_weight_words("w2_raw", H // 2, w2_words.rearrange("a p c -> p a c"))
         load_weight_words("w3_raw", H, w3_words.rearrange("a p c i -> p a (c i)"))
-        load_weight_scales("w2_scale_raw", w2_scales)
-        load_table(1)
-        clear_planes()
+        clear_planes(EARLY)
+        clear_planes(LATE)
+        reorder_scales(nc.scalar.copy, "w2_planes", "w2_scale_raw")
         reorder_words(nc.scalar.copy, "w2_codes", "w2_raw", RUN // 2)
         reorder_words(nc.scalar.copy, "w3_codes", "w3_raw", RUN)
-        reorder_scales(nc.scalar.copy, "w2_planes", "w2_scale_raw")
-        gather_scales()
-        place_planes()
+        gather_scales(EARLY)
+        place_planes(EARLY)
+        load_table(1)
+        gather_scales(LATE, below=12 * KIB, above=8 * KIB)
+        place_planes(LATE)
         load_w1(0, "scale_table", 64 - 8 * KIB)
         clear_weight_scales("w3_scale_raw", "scale_table", KIB)
         load_weight_scales("w3_scale_raw", w3_scales)
-        load_w1(1, "picked_scales", 64 - 8 * KIB)
+        load_w1(1, "picked_size", 64 - 8 * KIB)
         load_w4()
         load_bias()
 
@@ -321,15 +326,15 @@ def tile_list_sketch_cardinality_kernel(
         size(1, 2, "w1_raw1", 64 + 4 * KIB)
         gather_col(1, over="w1_grouped1")
         round_w4([scalar_round] * SLOTS)
-        col(0, 4)
-        col(1, 5)
+        col(0, 0)
+        col(1, 1)
         h_pair(0, below=2 * KIB, above=5 * KIB)
         smaller(0)
         times(nc.gpsimd, 0)
         smaller(1)
         times(nc.gpsimd, 1)
-        col(2, 0)
-        col(3, 1)
+        col(2, 6)
+        col(3, 7)
         gather_col(2, over="pred0")
         smaller(2)
         smaller(3)

@@ -67,8 +67,8 @@ def tile_list_sketch_cardinality_kernel(
             nc.sync.dma_start(tiles["list_" + name][:], src)
 
         def load_table_scales():
-            window = held("scale_table", [P, T // 4], I32, below=8 * KIB)
-            nc.gpsimd.memset(window[0:SCALE_ROW0, :], 0)
+            window = held("scale_table", [P, T // 4], I32, below=12 * KIB, above=KIB)
+            nc.vector.memset(window[0:SCALE_ROW0, :], 0)
             rows = tab_scales.bitcast(I32).rearrange("a (q r) c -> r q a c", r=4)
             for r in range(4):
                 nc.sync.dma_start(window[SCALE_ROW0 + r : P : 4, :], rows[r])
@@ -76,11 +76,11 @@ def tile_list_sketch_cardinality_kernel(
         def clear_weight_scales(name, over=None, at=0):
             nc.gpsimd.memset(held(name, [P, PASSES, H // 4], I32, over, at)[:], 0)
 
-        def load_weight_scales(name, src):
+        def load_weight_scales(queue, name, src):
             raw = tiles[name]
             rows = src.bitcast(I32).rearrange("a (q r) c -> q r a c", r=4)
             for q in range(4):
-                nc.sync.dma_start(raw[32 * q : 32 * q + 4], rows[q])
+                queue.dma_start(raw[32 * q : 32 * q + 4], rows[q])
 
         def load_weight_words(name, words, src, over=None, at=0):
             nc.sync.dma_start(held(name, [P, PASSES, words], I32, over, at)[:], src.bitcast(I32))
@@ -89,7 +89,7 @@ def tile_list_sketch_cardinality_kernel(
             src = tab_words[a].rearrange("p t i -> p (t i)").bitcast(I32)
             nc.sync.dma_start(held("word_table%d" % a, [P, T], I32)[:], src)
 
-        def load_w1(a, over, at):
+        def load_w1(a, over=None, at=0):
             rows = w1[512 * a : 512 * (a + 1), :].rearrange("(p s) c -> p s c", s=SLOTS)
             nc.sync.dma_start(held("w1_raw%d" % a, [P, SLOTS, H], F32, over, at)[:], rows)
 
@@ -101,7 +101,7 @@ def tile_list_sketch_cardinality_kernel(
 
         def load_bias():
             with nc.allow_non_contiguous_dma(reason="one bias value a partition"):
-                nc.sync.dma_start(held("bias", [P, N // P], F32, "scale_table", 2 * KIB)[:], b.rearrange("(t p) -> p t", p=P))
+                nc.sync.dma_start(held("bias", [P, N // P], F32, "scale_table", 3 * KIB)[:], b.rearrange("(t p) -> p t", p=P))
 
 
         def clear_planes(names):
@@ -113,9 +113,9 @@ def tile_list_sketch_cardinality_kernel(
             for u, name in enumerate(names):
                 nc.vector.tensor_copy(picked[:, u * S : (u + 1) * S], window.indirect(tiles["list_" + name][:]))
 
-        def reorder_scales(copy, name, raw):
+        def reorder_scales(copy, name, raw, over=None):
             words = RUN // 4
-            dst = held(name, [P, PASSES, H // 4], U32)
+            dst = held(name, [P, PASSES, H // 4], U32, over)
             copy(
                 dst[:].rearrange("p a (t g i) -> p a t g i", t=SLOTS, i=words),
                 tiles[raw][:].bitcast(U32).rearrange("p a (g t i) -> p a t g i", t=SLOTS, i=words),
@@ -284,23 +284,23 @@ def tile_list_sketch_cardinality_kernel(
         load_list("size", offs3)
         load_list("col", offs)
         load_table(0)
-        load_weight_scales("w2_scale_raw", w2_scales)
+        load_weight_scales(nc.sync, "w2_scale_raw", w2_scales)
         load_weight_words("w2_raw", H // 2, w2_words.rearrange("a p c -> p a c"))
         load_weight_words("w3_raw", H, w3_words.rearrange("a p c i -> p a (c i)"))
         clear_planes(EARLY)
         clear_planes(LATE)
+        clear_weight_scales("w3_scale_raw")
+        load_weight_scales(nc.gpsimd, "w3_scale_raw", w3_scales)
         reorder_scales(nc.scalar.copy, "w2_planes", "w2_scale_raw")
         reorder_words(nc.scalar.copy, "w2_codes", "w2_raw", RUN // 2)
         reorder_words(nc.scalar.copy, "w3_codes", "w3_raw", RUN)
         gather_scales(EARLY)
         place_planes(EARLY)
         load_table(1)
-        gather_scales(LATE, below=12 * KIB, above=8 * KIB)
+        load_w1(0)
+        gather_scales(LATE, above=8 * KIB)
         place_planes(LATE)
-        load_w1(0, "scale_table", 64 - 8 * KIB)
-        clear_weight_scales("w3_scale_raw", "scale_table", KIB)
-        load_weight_scales("w3_scale_raw", w3_scales)
-        load_w1(1, "picked_size", 64 - 8 * KIB)
+        load_w1(1, "scale_table", 64 - 8 * KIB)
         load_w4()
         load_bias()
 
@@ -314,7 +314,7 @@ def tile_list_sketch_cardinality_kernel(
         pred(1, 2)
         gather_half("size", 1, 1)
         gather_half("size", 1, 0, over="words_pred01")
-        reorder_scales(nc.scalar.copy, "w3_planes", "w3_scale_raw")
+        reorder_scales(nc.scalar.copy, "w3_planes", "w3_scale_raw", over="w3_raw")
         pred(2, 4)
         gather_col(0, over="words_pred11")
         round_w1(0, [pool_round] * SLOTS)
@@ -323,9 +323,9 @@ def tile_list_sketch_cardinality_kernel(
         quantize_w1(1)
         size(0, 0, "w1_raw1", 64 - 4 * KIB)
         pred(3, 6, "w1_raw1", 64)
-        size(1, 2, "w1_raw1", 64 + 4 * KIB)
-        gather_col(1, over="w1_grouped1")
-        round_w4([scalar_round] * SLOTS)
+        size(1, 2, "w1_raw1", 64 + 6 * KIB)
+        gather_col(1, over="w1_raw1", at=64 + 4 * KIB)
+        round_w4([pool_round, pool_round, scalar_round, scalar_round])
         col(0, 0)
         col(1, 1)
         h_pair(0, below=2 * KIB, above=5 * KIB)
@@ -335,7 +335,7 @@ def tile_list_sketch_cardinality_kernel(
         times(nc.gpsimd, 1)
         col(2, 6)
         col(3, 7)
-        gather_col(2, over="pred0")
+        gather_col(2, over="words_col0")
         smaller(2)
         smaller(3)
         size(2, 4, "w4_raw", 0)
@@ -357,7 +357,7 @@ def tile_list_sketch_cardinality_kernel(
         head(2, 2, 0)
         h_pair(2, over="h1", at=-64)
         times(nc.gpsimd, 4)
-        smaller(6, over="h1", at=2 * KIB - 64)
+        smaller(6, over="factor1")
         smaller(7)
         times(nc.vector, 5)
         quantize_h(4, 2)

@@ -230,16 +230,14 @@ def tile_list_sketch_cardinality_kernel(
             tiles["col%d" % chunk] = product("col", number, chunk * CHUNK, range(SLOTS))
 
         def smaller(chunk, over=None, at=0):
-            if chunk % 2 == 0:
-                held("smaller%d" % (chunk // 2), [P, 2, CHUNK, 2, 2], F32, over, at)
-            dst = tiles["smaller%d" % (chunk // 2)][:, chunk % 2]
+            dst = held("smaller%d" % chunk, [P, CHUNK, 2, 2], F32, over, at)[:]
             j0 = chunk % 2 * CHUNK
             other = tiles["pred%d" % (chunk // 2)][:, :, j0 : j0 + CHUNK, :].rearrange("p u j s -> p j u s")
             nc.vector.tensor_tensor(dst, tiles["col%d" % chunk].rearrange("p j (u s) -> p j u s", u=2), other, MIN)
 
         def times(engine, chunk):
             dst = tiles["h%d" % (chunk // 2)][:, chunk % 2]
-            src = tiles["smaller%d" % (chunk // 2)][:, chunk % 2].rearrange("p j u s -> p j (u s)")
+            src = tiles["smaller%d" % chunk][:].rearrange("p j u s -> p j (u s)")
             engine.tensor_tensor(dst, src, tiles["factor%d" % (chunk // 2)][:, chunk % 2], MULT)
 
         def h_pair(pair, over=None, at=0, below=0, above=0):
@@ -325,7 +323,7 @@ def tile_list_sketch_cardinality_kernel(
         pred(3, 6, "w1_raw1", 64)
         size(1, 2, "w1_raw1", 64 + 6 * KIB)
         gather_col(1, over="w1_raw1", at=64 + 4 * KIB)
-        round_w4([pool_round, pool_round, scalar_round, scalar_round])
+        round_w4([pool_round, scalar_round, scalar_round, scalar_round])
         col(0, 0)
         col(1, 1)
         h_pair(0, below=2 * KIB, above=5 * KIB)
@@ -340,7 +338,7 @@ def tile_list_sketch_cardinality_kernel(
         smaller(3)
         size(2, 4, "w4_raw", 0)
         size(3, 0, "w4_raw", 4 * KIB)
-        quantize("w4", tiles["w4_grouped"][:].rearrange("p t g i s -> p (t g i s)"), over="smaller0")
+        quantize("w4", tiles["w4_grouped"][:].rearrange("p t g i s -> p (t g i s)"), over="smaller1")
         quantize_h(0, 2, over="w4_grouped")
         col(4, 2)
         col(5, 3)
@@ -350,19 +348,19 @@ def tile_list_sketch_cardinality_kernel(
         times(nc.gpsimd, 2)
         times(nc.gpsimd, 3)
         smaller(4, over="w4_grouped", at=KIB)
-        smaller(5)
+        smaller(5, over="w4_grouped", at=3 * KIB)
         col(6, 4)
         col(7, 5)
+        smaller(6)
         quantize_h(2, 2)
         head(2, 2, 0)
-        h_pair(2, over="h1", at=-64)
-        times(nc.gpsimd, 4)
-        smaller(6, over="factor1")
-        smaller(7)
+        h_pair(2, over="factor1")
+        h_pair(3, over="smaller3")
+        times(nc.vector, 4)
         times(nc.vector, 5)
+        smaller(7, over="factor1", at=2 * KIB)
         quantize_h(4, 2)
         head(4, 2, 2)
-        h_pair(3)
         times(nc.vector, 6)
         times(nc.vector, 7)
         quantize_h(6, 1)

@@ -216,9 +216,9 @@ def tile_list_sketch_cardinality_kernel(
             return sums.rearrange("p t j -> p j t")
 
         def size(pair, number, over, at):
-            dst = held("factor%d" % pair, [P, 2, CHUNK, SLOTS], F32, over, at)
+            dst = held("factor%d" % pair, [P, 2, PAIR, 2], F32, over, at)
             for u in range(2):
-                sums = product("size", number + u, pair * PAIR + u * CHUNK, range(SLOTS))
+                sums = product("size", number + u, pair * PAIR, (2 * u, 2 * u + 1))
                 nc.scalar.activation(dst[:, u], sums, EXP)
 
         def pred(pair, number, over=None, at=0):
@@ -236,9 +236,10 @@ def tile_list_sketch_cardinality_kernel(
             nc.vector.tensor_tensor(dst, tiles["col%d" % chunk].rearrange("p j (u s) -> p j u s", u=2), other, MIN)
 
         def times(engine, chunk):
-            dst = tiles["h%d" % (chunk // 2)][:, chunk % 2]
-            src = tiles["smaller%d" % chunk][:].rearrange("p j u s -> p j (u s)")
-            engine.tensor_tensor(dst, src, tiles["factor%d" % (chunk // 2)][:, chunk % 2], MULT)
+            j0 = chunk % 2 * CHUNK
+            dst = tiles["h%d" % (chunk // 2)][:, chunk % 2].rearrange("p j (u s) -> p j u s", u=2)
+            factor = tiles["factor%d" % (chunk // 2)][:, :, j0 : j0 + CHUNK, :].rearrange("p u j s -> p j u s")
+            engine.tensor_tensor(dst, tiles["smaller%d" % chunk][:], factor, MULT)
 
         def h_pair(pair, over=None, at=0, below=0, above=0):
             held("h%d" % pair, [P, 2, CHUNK, SLOTS], BF16, over, at, below, above)
@@ -250,7 +251,7 @@ def tile_list_sketch_cardinality_kernel(
             h_part = tiles["h%d" % (chunk // 2)][:, chunk % 2 : chunk % 2 + count]
             quantize("hq%d" % chunk, h_part.rearrange("p u j t -> p (u j t)"), over)
 
-        def head(chunk, count, number):
+        def head(chunk, count, number, queue=nc.sync):
             width = count * CHUNK
             j0 = chunk * CHUNK
             group = SLOTS * CHUNK // width
@@ -274,7 +275,7 @@ def tile_list_sketch_cardinality_kernel(
                         bias = tiles["bias"][:, t0 + u : t0 + u + 1]
                         nc.scalar.activation(result[:, u, :], sums[:, u, :], EXP, bias=bias)
                     dst = out_view[:, t0 + rows.start : t0 + rows.stop, j0 : j0 + width]
-                    nc.sync.dma_start(dst, result[:, rows, :])
+                    queue.dma_start(dst, result[:, rows, :])
 
         clear_weight_scales("w2_scale_raw")
         load_list("pred", offs2)
@@ -366,4 +367,4 @@ def tile_list_sketch_cardinality_kernel(
         quantize_h(6, 1)
         head(6, 1, 6)
         quantize_h(7, 1)
-        head(7, 1, 7)
+        head(7, 1, 7, nc.scalar)

@@ -32,8 +32,6 @@ PAIR = 2 * CHUNK
 KIB = 1024
 STORE_ROWS = 2
 SCALE_ROW0 = P - PASSES * BLOCKS
-EARLY = ("pred",)
-LATE = ("size", "col")
 
 
 def tile_list_sketch_cardinality_kernel(
@@ -67,7 +65,7 @@ def tile_list_sketch_cardinality_kernel(
             nc.sync.dma_start(tiles["list_" + name][:], src)
 
         def load_table_scales():
-            window = held("scale_table", [P, T // 4], I32, below=12 * KIB, above=KIB)
+            window = held("scale_table", [P, T // 4], I32, below=12 * KIB, above=9 * KIB)
             nc.vector.memset(window[0:SCALE_ROW0, :], 0)
             rows = tab_scales.bitcast(I32).rearrange("a (q r) c -> r q a c", r=4)
             for r in range(4):
@@ -94,24 +92,22 @@ def tile_list_sketch_cardinality_kernel(
             nc.sync.dma_start(held("w1_raw%d" % a, [P, SLOTS, H], F32, over, at)[:], rows)
 
         def load_w4():
-            raw = held("w4_raw", [P, SLOTS, N], F32, "picked_size", 2 * KIB - 64)
+            raw = held("w4_raw", [P, SLOTS, N], F32, "scale_table", 4 * KIB - 64)
             rows = w4.rearrange("(g t i) n -> t g i n", t=SLOTS, i=RUN)
             for t in range(SLOTS):
                 nc.sync.dma_start(raw[:, t, :], rows[t])
 
         def load_bias():
             with nc.allow_non_contiguous_dma(reason="one bias value a partition"):
-                nc.sync.dma_start(held("bias", [P, N // P], F32, "scale_table", 3 * KIB)[:], b.rearrange("(t p) -> p t", p=P))
+                nc.sync.dma_start(held("bias", [P, N // P], F32, "picked_col")[:], b.rearrange("(t p) -> p t", p=P))
 
 
-        def clear_planes(names):
-            nc.gpsimd.memset(held("planes_" + names[0], [P, PASSES * len(names) * S // 4], I32)[:], 0)
+        def clear_planes(name):
+            nc.gpsimd.memset(held("planes_" + name, [P, PASSES * S // 4], I32)[:], 0)
 
-        def gather_scales(names, below=0, above=0):
+        def gather_scales(name):
             window = tiles["scale_table"][:].bitcast(U8)
-            picked = held("picked_" + names[0], [P, len(names) * S], U8, below=below, above=above)
-            for u, name in enumerate(names):
-                nc.vector.tensor_copy(picked[:, u * S : (u + 1) * S], window.indirect(tiles["list_" + name][:]))
+            nc.vector.tensor_copy(held("picked_" + name, [P, S], U8)[:], window.indirect(tiles["list_" + name][:]))
 
         def reorder_scales(copy, name, raw, over=None):
             words = RUN // 4
@@ -121,16 +117,14 @@ def tile_list_sketch_cardinality_kernel(
                 tiles[raw][:].bitcast(U32).rearrange("p a (g t i) -> p a t g i", t=SLOTS, i=words),
             )
 
-        def place_planes(names):
-            picked = tiles["picked_" + names[0]][:].bitcast(I32)
+        def place_planes(name):
+            picked = tiles["picked_" + name][:].bitcast(I32)
             for r in range(4):
-                dst = tiles["planes_" + names[0]][r:P:32, :].rearrange("p (a c) -> p a c", a=PASSES)
+                dst = tiles["planes_" + name][r:P:32, :].rearrange("p (a c) -> p a c", a=PASSES)
                 nc.sync.dma_start(dst, picked[SCALE_ROW0 + r : P : 4, :])
 
         def plane(name, a, j0, width):
-            names = EARLY if name in EARLY else LATE
-            col0 = (a * len(names) + names.index(name)) * S + j0
-            return tiles["planes_" + names[0]][:].bitcast(U8)[:, col0 : col0 + width]
+            return tiles["planes_" + name][:].bitcast(U8)[:, a * S + j0 : a * S + j0 + width]
 
         def weight_plane(name, a, t):
             return tiles[name][:, a].bitcast(U8)[:, t * P : (t + 1) * P]
@@ -149,6 +143,11 @@ def tile_list_sketch_cardinality_kernel(
 
         def gather_half(name, half, a, over=None, at=0, spare=0):
             gather(held("words_%s%d%d" % (name, half, a), [P, HALF], U32, over, at, spare, spare)[:], name, half * HALF, HALF, a)
+
+        def gather_half_by_pairs(name, half, a):
+            dst = held("words_%s%d%d" % (name, half, a), [P, HALF], U32)
+            for j0 in range(0, HALF, PAIR):
+                gather(dst[:, j0 : j0 + PAIR], name, half * HALF + j0, PAIR, a)
 
         def gather_col(pair, over, at=0):
             dst = held("words_col%d" % pair, [P, PASSES, PAIR], U32, over, at)
@@ -177,8 +176,8 @@ def tile_list_sketch_cardinality_kernel(
         def round_w1(a, copies, above=0):
             grouped = held("w1_grouped%d" % a, [P, SLOTS, BLOCKS, RUN, SLOTS], BF16, above=above)
             src = tiles["w1_raw%d" % a][:].rearrange("p s (g t i) -> p t g i s", t=SLOTS, i=RUN)
-            for t, copy in enumerate(copies):
-                copy(grouped[:, t], src[:, t])
+            for t, blocks, copy in copies:
+                copy(grouped[:, t, blocks], src[:, t, blocks])
 
         def quantize_w1(a):
             quantize("w1_%d" % a, tiles["w1_grouped%d" % a][:].rearrange("p t g i s -> p (t g i s)"))
@@ -251,17 +250,18 @@ def tile_list_sketch_cardinality_kernel(
             h_part = tiles["h%d" % (chunk // 2)][:, chunk % 2 : chunk % 2 + count]
             quantize("hq%d" % chunk, h_part.rearrange("p u j t -> p (u j t)"), over)
 
-        def head(chunk, count, number, queue=nc.sync):
+        def head(chunk, count, numbers, queue=nc.sync):
             width = count * CHUNK
             j0 = chunk * CHUNK
-            group = SLOTS * CHUNK // width
-            for t0 in range(0, N // P, group):
-                sums = bank(number + t0 // group, "last")[:].rearrange("p (u j) -> p u j", j=width)
-                result = held("result%d_%d" % (chunk, t0), [P, group, width], F32)
+            group = N // P // len(numbers)
+            sums = []
+            for number in numbers:
+                opened = bank(number, "last")
                 for u in range(group):
-                    cols = slice((t0 + u) * P, (t0 + u + 1) * P)
+                    cols = slice(len(sums) * P, (len(sums) + 1) * P)
+                    sums.append(opened[:, u * width : (u + 1) * width])
                     nc.tensor.matmul_mx(
-                        out=sums[:, u, :],
+                        out=sums[-1],
                         lhsT=tiles["w4_codes"][:, cols].bitcast(FP8X4),
                         lhsT_scale=tiles["w4_scales"][:, cols],
                         rhs=tiles["hq%d_codes" % chunk][:].bitcast(FP8X4),
@@ -269,13 +269,12 @@ def tile_list_sketch_cardinality_kernel(
                         start=True,
                         stop=True,
                     )
-                for u0 in range(0, group, STORE_ROWS):
-                    rows = slice(u0, u0 + STORE_ROWS)
-                    for u in range(rows.start, rows.stop):
-                        bias = tiles["bias"][:, t0 + u : t0 + u + 1]
-                        nc.scalar.activation(result[:, u, :], sums[:, u, :], EXP, bias=bias)
-                    dst = out_view[:, t0 + rows.start : t0 + rows.stop, j0 : j0 + width]
-                    queue.dma_start(dst, result[:, rows, :])
+            for t0 in range(0, N // P, STORE_ROWS):
+                result = held("result%d_%d" % (chunk, t0), [P, STORE_ROWS, width], F32)
+                for u in range(STORE_ROWS):
+                    bias = tiles["bias"][:, t0 + u : t0 + u + 1]
+                    nc.scalar.activation(result[:, u, :], sums[t0 + u], EXP, bias=bias)
+                queue.dma_start(out_view[:, t0 : t0 + STORE_ROWS, j0 : j0 + width], result[:])
 
         clear_weight_scales("w2_scale_raw")
         load_list("pred", offs2)
@@ -286,27 +285,29 @@ def tile_list_sketch_cardinality_kernel(
         load_weight_scales(nc.sync, "w2_scale_raw", w2_scales)
         load_weight_words("w2_raw", H // 2, w2_words.rearrange("a p c -> p a c"))
         load_weight_words("w3_raw", H, w3_words.rearrange("a p c i -> p a (c i)"))
-        clear_planes(EARLY)
-        clear_planes(LATE)
+        for name in ("pred", "size", "col"):
+            clear_planes(name)
         clear_weight_scales("w3_scale_raw")
         load_weight_scales(nc.gpsimd, "w3_scale_raw", w3_scales)
         reorder_scales(nc.scalar.copy, "w2_planes", "w2_scale_raw")
         reorder_words(nc.scalar.copy, "w2_codes", "w2_raw", RUN // 2)
         reorder_words(nc.scalar.copy, "w3_codes", "w3_raw", RUN)
-        gather_scales(EARLY)
-        place_planes(EARLY)
+        gather_scales("pred")
+        place_planes("pred")
         load_table(1)
         load_w1(0)
-        gather_scales(LATE, above=8 * KIB)
-        place_planes(LATE)
+        gather_scales("size")
+        place_planes("size")
+        gather_scales("col")
         load_w1(1, "scale_table", 64 - 8 * KIB)
         load_w4()
+        place_planes("col")
         load_bias()
 
         gather_half("pred", 0, 0)
         gather_half("pred", 1, 0)
         gather_half("size", 0, 0)
-        gather_half("pred", 0, 1)
+        gather_half_by_pairs("pred", 0, 1)
         gather_half("pred", 1, 1)
         gather_half("size", 0, 1)
         pred(0, 0)
@@ -316,15 +317,16 @@ def tile_list_sketch_cardinality_kernel(
         reorder_scales(nc.scalar.copy, "w3_planes", "w3_scale_raw", over="w3_raw")
         pred(2, 4)
         gather_col(0, over="words_pred11")
-        round_w1(0, [pool_round] * SLOTS)
-        round_w1(1, [scalar_round, scalar_round, scalar_round, pool_round], above=3 * KIB)
+        whole = slice(0, BLOCKS)
+        round_w1(0, [(t, whole, pool_round) for t in range(SLOTS)])
+        round_w1(1, [(t, whole, scalar_round) for t in range(SLOTS)], above=3 * KIB)
         quantize_w1(0)
         quantize_w1(1)
         size(0, 0, "w1_raw1", 64 - 4 * KIB)
         pred(3, 6, "w1_raw1", 64)
-        size(1, 2, "w1_raw1", 64 + 6 * KIB)
         gather_col(1, over="w1_raw1", at=64 + 4 * KIB)
         round_w4([pool_round, scalar_round, scalar_round, scalar_round])
+        size(1, 2, "w4_raw", 64 - 4 * KIB)
         col(0, 0)
         col(1, 1)
         h_pair(0, below=2 * KIB, above=5 * KIB)
@@ -337,13 +339,13 @@ def tile_list_sketch_cardinality_kernel(
         gather_col(2, over="words_col0")
         smaller(2)
         smaller(3)
-        size(2, 4, "w4_raw", 0)
-        size(3, 0, "w4_raw", 4 * KIB)
+        size(2, 4, "w4_raw", 64)
+        size(3, 0, "w4_raw", 64 + 4 * KIB)
         quantize("w4", tiles["w4_grouped"][:].rearrange("p t g i s -> p (t g i s)"), over="smaller1")
         quantize_h(0, 2, over="w4_grouped")
         col(4, 2)
         col(5, 3)
-        head(0, 2, 6)
+        head(0, 2, [6, 7])
         gather_col(3, over="h0", at=64 - 2 * KIB)
         h_pair(1, over="h0", at=128)
         times(nc.gpsimd, 2)
@@ -354,17 +356,17 @@ def tile_list_sketch_cardinality_kernel(
         col(7, 5)
         smaller(6)
         quantize_h(2, 2)
-        head(2, 2, 0)
+        head(2, 2, [0, 1])
         h_pair(2, over="factor1")
         h_pair(3, over="smaller3")
         times(nc.vector, 4)
         times(nc.vector, 5)
         smaller(7, over="factor1", at=2 * KIB)
         quantize_h(4, 2)
-        head(4, 2, 2)
+        head(4, 2, [2, 3, 4, 5])
         times(nc.vector, 6)
         times(nc.vector, 7)
         quantize_h(6, 1)
-        head(6, 1, 6)
+        head(6, 1, [6, 7, 0, 1])
         quantize_h(7, 1)
-        head(7, 1, 7, nc.scalar)
+        head(7, 1, [2, 3, 4, 5], nc.scalar)

@@ -69,7 +69,7 @@ def tile_list_sketch_cardinality_kernel(
             nc.vector.memset(window[0:SCALE_ROW0, :], 0)
             rows = tab_scales.bitcast(I32).rearrange("a (q r) c -> r q a c", r=4)
             for r in range(4):
-                nc.sync.dma_start(window[SCALE_ROW0 + r : P : 4, :], rows[r])
+                (nc.sync, nc.scalar)[r % 2].dma_start(window[SCALE_ROW0 + r : P : 4, :], rows[r])
 
         def clear_weight_scales(name, over=None, at=0):
             nc.gpsimd.memset(held(name, [P, PASSES, H // 4], I32, over, at)[:], 0)
@@ -144,10 +144,8 @@ def tile_list_sketch_cardinality_kernel(
         def gather_half(name, half, a, over=None, at=0, spare=0):
             gather(held("words_%s%d%d" % (name, half, a), [P, HALF], U32, over, at, spare, spare)[:], name, half * HALF, HALF, a)
 
-        def gather_half_by_pairs(name, half, a):
-            dst = held("words_%s%d%d" % (name, half, a), [P, HALF], U32)
-            for j0 in range(0, HALF, PAIR):
-                gather(dst[:, j0 : j0 + PAIR], name, half * HALF + j0, PAIR, a)
+        def gather_pair(name, pair, a):
+            gather(held("words_%s_pair%d%d" % (name, pair, a), [P, PAIR], U32)[:], name, pair * PAIR, PAIR, a)
 
         def gather_col(pair, over, at=0):
             dst = held("words_col%d" % pair, [P, PASSES, PAIR], U32, over, at)
@@ -157,6 +155,8 @@ def tile_list_sketch_cardinality_kernel(
         def words(name, j0, width, a):
             if name == "col":
                 return tiles["words_col%d" % (j0 // PAIR)][:, a, j0 % PAIR : j0 % PAIR + width]
+            if "words_%s_pair%d%d" % (name, j0 // PAIR, a) in tiles:
+                return tiles["words_%s_pair%d%d" % (name, j0 // PAIR, a)][:]
             return tiles["words_%s%d%d" % (name, j0 // HALF, a)][:, j0 % HALF : j0 % HALF + width]
 
         def pool_round(dst, src):
@@ -250,7 +250,7 @@ def tile_list_sketch_cardinality_kernel(
             h_part = tiles["h%d" % (chunk // 2)][:, chunk % 2 : chunk % 2 + count]
             quantize("hq%d" % chunk, h_part.rearrange("p u j t -> p (u j t)"), over)
 
-        def head(chunk, count, numbers, queue=nc.sync):
+        def head(chunk, count, numbers, stores=((0, 2, nc.sync), (2, 4, nc.sync))):
             width = count * CHUNK
             j0 = chunk * CHUNK
             group = N // P // len(numbers)
@@ -269,16 +269,15 @@ def tile_list_sketch_cardinality_kernel(
                         start=True,
                         stop=True,
                     )
-            for t0 in range(0, N // P, STORE_ROWS):
-                result = held("result%d_%d" % (chunk, t0), [P, STORE_ROWS, width], F32)
-                for u in range(STORE_ROWS):
-                    bias = tiles["bias"][:, t0 + u : t0 + u + 1]
-                    nc.scalar.activation(result[:, u, :], sums[t0 + u], EXP, bias=bias)
-                queue.dma_start(out_view[:, t0 : t0 + STORE_ROWS, j0 : j0 + width], result[:])
+            for t0, t1, queue in stores:
+                result = held("result%d_%d" % (chunk, t0), [P, t1 - t0, width], F32)
+                for t in range(t0, t1):
+                    nc.scalar.activation(result[:, t - t0, :], sums[t], EXP, bias=tiles["bias"][:, t : t + 1])
+                queue.dma_start(out_view[:, t0:t1, j0 : j0 + width], result[:])
 
         clear_weight_scales("w2_scale_raw")
-        load_list("pred", offs2)
         load_table_scales()
+        load_list("pred", offs2)
         load_list("size", offs3)
         load_list("col", offs)
         load_table(0)
@@ -307,14 +306,15 @@ def tile_list_sketch_cardinality_kernel(
         gather_half("pred", 0, 0)
         gather_half("pred", 1, 0)
         gather_half("size", 0, 0)
-        gather_half_by_pairs("pred", 0, 1)
+        gather_pair("pred", 0, 1)
+        gather_pair("pred", 1, 1)
         gather_half("pred", 1, 1)
         gather_half("size", 0, 1)
         pred(0, 0)
         pred(1, 2)
         gather_half("size", 1, 1)
-        gather_half("size", 1, 0, over="words_pred01")
-        reorder_scales(nc.scalar.copy, "w3_planes", "w3_scale_raw", over="w3_raw")
+        gather_half("size", 1, 0, over="words_pred_pair01")
+        reorder_scales(nc.gpsimd.tensor_copy, "w3_planes", "w3_scale_raw")
         pred(2, 4)
         gather_col(0, over="words_pred11")
         whole = slice(0, BLOCKS)
@@ -342,16 +342,16 @@ def tile_list_sketch_cardinality_kernel(
         size(2, 4, "w4_raw", 64)
         size(3, 0, "w4_raw", 64 + 4 * KIB)
         quantize("w4", tiles["w4_grouped"][:].rearrange("p t g i s -> p (t g i s)"), over="smaller1")
-        quantize_h(0, 2, over="w4_grouped")
+        quantize_h(0, 2)
         col(4, 2)
         col(5, 3)
         head(0, 2, [6, 7])
         gather_col(3, over="h0", at=64 - 2 * KIB)
-        h_pair(1, over="h0", at=128)
+        h_pair(1, over="w4_grouped")
         times(nc.gpsimd, 2)
         times(nc.gpsimd, 3)
-        smaller(4, over="w4_grouped", at=KIB)
-        smaller(5, over="w4_grouped", at=3 * KIB)
+        smaller(4, over="w4_grouped", at=2 * KIB)
+        smaller(5, over="h0", at=64)
         col(6, 4)
         col(7, 5)
         smaller(6)
@@ -361,12 +361,14 @@ def tile_list_sketch_cardinality_kernel(
         h_pair(3, over="smaller3")
         times(nc.vector, 4)
         times(nc.vector, 5)
-        smaller(7, over="factor1", at=2 * KIB)
-        quantize_h(4, 2)
-        head(4, 2, [2, 3, 4, 5])
+        quantize_h(4, 1)
+        head(4, 1, [2, 3])
         times(nc.vector, 6)
-        times(nc.vector, 7)
+        quantize_h(5, 1)
+        head(5, 1, [4, 6])
+        smaller(7, over="factor1", at=2 * KIB)
         quantize_h(6, 1)
-        head(6, 1, [6, 7, 0, 1])
+        head(6, 1, [7, 0])
+        times(nc.vector, 7)
         quantize_h(7, 1)
-        head(7, 1, [2, 3, 4, 5], nc.scalar)
+        head(7, 1, [1, 2, 3, 5], ((0, 2, nc.sync), (2, 3, nc.sync), (3, 4, nc.scalar)))

@@ -144,8 +144,8 @@ def tile_list_sketch_cardinality_kernel(
         def gather_half(name, half, a, over=None, at=0, spare=0):
             gather(held("words_%s%d%d" % (name, half, a), [P, HALF], U32, over, at, spare, spare)[:], name, half * HALF, HALF, a)
 
-        def gather_pair(name, pair, a):
-            gather(held("words_%s_pair%d%d" % (name, pair, a), [P, PAIR], U32)[:], name, pair * PAIR, PAIR, a)
+        def gather_pair(name, pair, a, over=None):
+            gather(held("words_%s_pair%d%d" % (name, pair, a), [P, PAIR], U32, over)[:], name, pair * PAIR, PAIR, a)
 
         def gather_col(pair, over, at=0):
             dst = held("words_col%d" % pair, [P, PASSES, PAIR], U32, over, at)
@@ -153,10 +153,10 @@ def tile_list_sketch_cardinality_kernel(
                 gather(dst[:, a, :], "col", pair * PAIR, PAIR, a)
 
         def words(name, j0, width, a):
+            if "words_%s_pair%d%d" % (name, j0 // PAIR, a) in tiles:
+                return tiles["words_%s_pair%d%d" % (name, j0 // PAIR, a)][:, j0 % PAIR : j0 % PAIR + width]
             if name == "col":
                 return tiles["words_col%d" % (j0 // PAIR)][:, a, j0 % PAIR : j0 % PAIR + width]
-            if "words_%s_pair%d%d" % (name, j0 // PAIR, a) in tiles:
-                return tiles["words_%s_pair%d%d" % (name, j0 // PAIR, a)][:]
             return tiles["words_%s%d%d" % (name, j0 // HALF, a)][:, j0 % HALF : j0 % HALF + width]
 
         def pool_round(dst, src):
@@ -306,6 +306,7 @@ def tile_list_sketch_cardinality_kernel(
         gather_half("pred", 0, 0)
         gather_half("pred", 1, 0)
         gather_half("size", 0, 0)
+        gather_pair("col", 0, 0)
         gather_pair("pred", 0, 1)
         gather_pair("pred", 1, 1)
         gather_half("pred", 1, 1)
@@ -316,7 +317,7 @@ def tile_list_sketch_cardinality_kernel(
         gather_half("size", 1, 0, over="words_pred_pair01")
         reorder_scales(nc.gpsimd.tensor_copy, "w3_planes", "w3_scale_raw")
         pred(2, 4)
-        gather_col(0, over="words_pred11")
+        gather_pair("col", 0, 1, over="words_pred11")
         whole = slice(0, BLOCKS)
         round_w1(0, [(t, whole, pool_round) for t in range(SLOTS)])
         round_w1(1, [(t, whole, scalar_round) for t in range(SLOTS)], above=3 * KIB)
@@ -336,7 +337,7 @@ def tile_list_sketch_cardinality_kernel(
         times(nc.gpsimd, 1)
         col(2, 6)
         col(3, 7)
-        gather_col(2, over="words_col0")
+        gather_col(2, over="words_col_pair01")
         smaller(2)
         smaller(3)
         size(2, 4, "w4_raw", 64)

@@ -166,6 +166,10 @@ def tile_list_sketch_cardinality_kernel(
             by_line = "p g (u i) s -> p g u s i"
             nc.scalar.copy(dst.rearrange(by_line, i=LINE), src.rearrange(by_line, i=LINE))
 
+        def vector_round(dst, src):
+            by_line = "p g (u i) s -> p g u s i"
+            nc.vector.tensor_copy(dst.rearrange(by_line, i=LINE), src.rearrange(by_line, i=LINE))
+
         def quantize(name, grouped_flat, over=None):
             width = grouped_flat.shape[1] // SLOTS
             codes = held(name + "_codes", [P, width], U32, over)
@@ -174,10 +178,14 @@ def tile_list_sketch_cardinality_kernel(
             return codes, scales
 
         def round_w1(a, copies, above=0):
-            grouped = held("w1_grouped%d" % a, [P, SLOTS, BLOCKS, RUN, SLOTS], BF16, above=above)
+            grouped = held("w1_grouped%d" % a, [P, len(copies), BLOCKS, RUN, SLOTS], BF16, above=above)
             src = tiles["w1_raw%d" % a][:].rearrange("p s (g t i) -> p t g i s", t=SLOTS, i=RUN)
             for t, blocks, copy in copies:
                 copy(grouped[:, t, blocks], src[:, t, blocks])
+
+        def round_w1_last_slot(over, at):
+            grouped = held("w1_grouped_last", [P, BLOCKS, RUN, SLOTS], BF16, over, at)
+            vector_round(grouped[:], tiles["w1_raw0"][:].rearrange("p s (g t i) -> p t g i s", t=SLOTS, i=RUN)[:, SLOTS - 1])
 
         def quantize_w1(a):
             quantize("w1_%d" % a, tiles["w1_grouped%d" % a][:].rearrange("p t g i s -> p (t g i s)"))
@@ -193,6 +201,8 @@ def tile_list_sketch_cardinality_kernel(
                 return tiles["w3_codes"][:, t, a, :].bitcast(FP8X4), weight_plane("w3_planes", a, t)
             if name == "pred":
                 return tiles["w2_codes"][:, t, a, :].bitcast(U8).bitcast(FP4X4), weight_plane("w2_planes", a, t)
+            if (a, t) == (0, SLOTS - 1):
+                return tiles["w1_last_codes"][:].bitcast(FP8X4), tiles["w1_last_scales"][:]
             cols = slice(t * P, (t + 1) * P)
             return tiles["w1_%d_codes" % a][:, cols].bitcast(FP8X4), tiles["w1_%d_scales" % a][:, cols]
 
@@ -319,9 +329,11 @@ def tile_list_sketch_cardinality_kernel(
         pred(2, 4)
         gather_pair("col", 0, 1, over="words_pred11")
         whole = slice(0, BLOCKS)
-        round_w1(0, [(t, whole, pool_round) for t in range(SLOTS)])
+        round_w1(0, [(t, whole, pool_round) for t in range(3)])
+        round_w1_last_slot("words_pred11", KIB)
         round_w1(1, [(t, whole, scalar_round) for t in range(SLOTS)], above=3 * KIB)
         quantize_w1(0)
+        quantize("w1_last", tiles["w1_grouped_last"][:].rearrange("p g i s -> p (g i s)"))
         quantize_w1(1)
         size(0, 0, "w1_raw1", 64 - 4 * KIB)
         pred(3, 6, "w1_raw1", 64)

import math
from contextlib import ExitStack

import concourse.mybir as mybir

K, T, S, H, N = 1024, 4096, 1024, 512, 512
FLOPS = 2 * (3 * K * H * S + H * N * S)

F32 = mybir.dt.float32
BF16 = mybir.dt.bfloat16
I32 = mybir.dt.int32
U32 = mybir.dt.uint32
U16 = mybir.dt.uint16
U8 = mybir.dt.uint8
NBYTES = {F32: 4, BF16: 2, I32: 4, U32: 4, U8: 1}
FP8X4 = mybir.dt.float8_e4m3fn_x4
FP4X4 = mybir.dt.float4_e2m1fn_x4
EXP = mybir.ActivationFunctionType.Exp
MIN = mybir.AluOpType.min
MULT = mybir.AluOpType.mult
ADD = mybir.AluOpType.add

P = 128
PASSES = K // 512
SLOTS = 4
RUN = 8
LINE = 4
BLOCKS = 16
HALF = S // 2
CHUNK = 128
PAIR = 2 * CHUNK
KIB = 1024
STORE_ROWS = 2
SCALE_ROW0 = P - PASSES * BLOCKS


def tile_list_sketch_cardinality_kernel(
    tc, tab_words, tab_scales, offs, offs2, offs3, w1, w2_words, w2_scales, w3_words, w3_scales, w4, b, out
):
    nc = tc.nc
    with ExitStack() as ctx:
        lists = ctx.enter_context(tc.tile_pool(name="lists", bufs=1))
        work = ctx.enter_context(tc.tile_pool(name="work", bufs=1))
        psum = ctx.enter_context(tc.psum_pool(name="psum", bufs=1))
        tiles = {}
        start = {}
        ends = [0]

        def held(name, shape, dtype, over=None, at=0, below=0, above=0):
            if over is None:
                start[name] = ends[-1] + below
                ends.append(start[name] + math.prod(shape[1:]) * NBYTES[dtype] + above)
                ends[-1] = (ends[-1] + 63) // 64 * 64
            else:
                start[name] = start[over] + at
            tiles[name] = work.tile(shape, dtype, name=name, tag=name, align_bytes=64, offset=start[name])
            return tiles[name]

        def bank(number, role):
            return psum.tile([P, SLOTS * CHUNK], F32, name=role, tag="bank%d" % number)


        def load_list(name, src):
            tiles["list_" + name] = lists.tile([P, S // 16], U16, name="list_" + name, tag="list_" + name)
            nc.sync.dma_start(tiles["list_" + name][:], src)

        def load_table_scales():
            window = held("scale_table", [P, T // 4], I32, below=12 * KIB, above=9 * KIB)
            nc.vector.memset(window[0:SCALE_ROW0, :], 0)
            rows = tab_scales.bitcast(I32).rearrange("a (q r) c -> r q a c", r=4)
            for r in range(4):
                (nc.sync, nc.scalar)[r % 2].dma_start(window[SCALE_ROW0 + r : P : 4, :], rows[r])

        def clear_weight_scales(name, over=None, at=0):
            nc.gpsimd.memset(held(name, [P, PASSES, H // 4], I32, over, at)[:], 0)

        def load_weight_scales(queue, name, src):
            raw = tiles[name]
            rows = src.bitcast(I32).rearrange("a (q r) c -> q r a c", r=4)
            for q in range(4):
                queue.dma_start(raw[32 * q : 32 * q + 4], rows[q])

        def load_weight_words(name, words, src, over=None, at=0):
            nc.sync.dma_start(held(name, [P, PASSES, words], I32, over, at)[:], src.bitcast(I32))

        def load_table(a):
            src = tab_words[a].rearrange("p t i -> p (t i)").bitcast(I32)
            nc.sync.dma_start(held("word_table%d" % a, [P, T], I32)[:], src)

        def load_w1(a, over=None, at=0):
            rows = w1[512 * a : 512 * (a + 1), :].rearrange("(p s) c -> p s c", s=SLOTS)
            nc.sync.dma_start(held("w1_raw%d" % a, [P, SLOTS, H], F32, over, at)[:], rows)

        def load_w4():
            raw = held("w4_raw", [P, SLOTS, N], F32, "scale_table", 4 * KIB - 64)
            rows = w4.rearrange("(g t i) n -> t g i n", t=SLOTS, i=RUN)
            for t in range(SLOTS):
                nc.sync.dma_start(raw[:, t, :], rows[t])

        def load_bias():
            with nc.allow_non_contiguous_dma(reason="one bias value a partition"):
                nc.sync.dma_start(held("bias", [P, N // P], F32, "picked_col")[:], b.rearrange("(t p) -> p t", p=P))


        def clear_planes(name):
            nc.gpsimd.memset(held("planes_" + name, [P, PASSES * S // 4], I32)[:], 0)

        def gather_scales(name):
            window = tiles["scale_table"][:].bitcast(U8)
            nc.vector.tensor_copy(held("picked_" + name, [P, S], U8)[:], window.indirect(tiles["list_" + name][:]))

        def reorder_scales(copy, name, raw, over=None):
            words = RUN // 4
            dst = held(name, [P, PASSES, H // 4], U32, over)
            copy(
                dst[:].rearrange("p a (t g i) -> p a t g i", t=SLOTS, i=words),
                tiles[raw][:].bitcast(U32).rearrange("p a (g t i) -> p a t g i", t=SLOTS, i=words),
            )

        def place_planes(name):
            picked = tiles["picked_" + name][:].bitcast(I32)
            for r in range(4):
                dst = tiles["planes_" + name][r:P:32, :].rearrange("p (a c) -> p a c", a=PASSES)
                nc.sync.dma_start(dst, picked[SCALE_ROW0 + r : P : 4, :])

        def plane(name, a, j0, width):
            return tiles["planes_" + name][:].bitcast(U8)[:, a * S + j0 : a * S + j0 + width]

        def weight_plane(name, a, t):
            return tiles[name][:, a].bitcast(U8)[:, t * P : (t + 1) * P]


        def reorder_words(copy, name, raw, words):
            dst = held(name, [P, SLOTS, PASSES, BLOCKS * words], U32)
            copy(
                dst[:].rearrange("p t a (g i) -> p t (a g) i", i=words),
                tiles[raw][:].bitcast(U32).rearrange("p a (g t i) -> p t (a g) i", t=SLOTS, i=words),
            )

        def gather(dst, name, j0, count, a):
            window = tiles["word_table%d" % a][:].bitcast(U32)
            nc.vector.tensor_copy(dst, window.indirect(tiles["list_" + name][:, j0 // 16 : (j0 + count) // 16]))

        def gather_half(name, half, a, over=None, at=0, spare=0):
            gather(held("words_%s%d%d" % (name, half, a), [P, HALF], U32, over, at, spare, spare)[:], name, half * HALF, HALF, a)

        def gather_pair(name, pair, a, over=None):
            gather(held("words_%s_pair%d%d" % (name, pair, a), [P, PAIR], U32, over)[:], name, pair * PAIR, PAIR, a)

        def gather_col(pair, over, at=0):
            dst = held("words_col%d" % pair, [P, PASSES, PAIR], U32, over, at)
            for a in range(PASSES):
                gather(dst[:, a, :], "col", pair * PAIR, PAIR, a)

        def words(name, j0, width, a):
            if "words_%s_pair%d%d" % (name, j0 // PAIR, a) in tiles:
                return tiles["words_%s_pair%d%d" % (name, j0 // PAIR, a)][:, j0 % PAIR : j0 % PAIR + width]
            if name == "col":
                return tiles["words_col%d" % (j0 // PAIR)][:, a, j0 % PAIR : j0 % PAIR + width]
            return tiles["words_%s%d%d" % (name, j0 // HALF, a)][:, j0 % HALF : j0 % HALF + width]

        def pool_round(dst, src):
            nc.gpsimd.tensor_scalar(dst, src, 1.0, 0.0, MULT, ADD)

        def scalar_round(dst, src):
            by_line = "p g (u i) s -> p g u s i"
            nc.scalar.copy(dst.rearrange(by_line, i=LINE), src.rearrange(by_line, i=LINE))

        def vector_round(dst, src):
            by_line = "p g (u i) s -> p g u s i"
            nc.vector.tensor_copy(dst.rearrange(by_line, i=LINE), src.rearrange(by_line, i=LINE))

        def quantize(name, grouped_flat, over=None):
            width = grouped_flat.shape[1] // SLOTS
            codes = held(name + "_codes", [P, width], U32, over)
            scales = held(name + "_scales", [P, width], U8)
            nc.vector.quantize_mx(out=codes[:].bitcast(FP8X4), scales=scales[:], in_=grouped_flat)
            return codes, scales

        def round_w1(a, copies, above=0):
            grouped = held("w1_grouped%d" % a, [P, len(copies), BLOCKS, RUN, SLOTS], BF16, above=above)
            src = tiles["w1_raw%d" % a][:].rearrange("p s (g t i) -> p t g i s", t=SLOTS, i=RUN)
            for t, blocks, copy in copies:
                copy(grouped[:, t, blocks], src[:, t, blocks])

        def round_w1_last_slot(over, at):
            grouped = held("w1_grouped_last", [P, BLOCKS, RUN, SLOTS], BF16, over, at)
            vector_round(grouped[:], tiles["w1_raw0"][:].rearrange("p s (g t i) -> p t g i s", t=SLOTS, i=RUN)[:, SLOTS - 1])

        def quantize_w1(a):
            quantize("w1_%d" % a, tiles["w1_grouped%d" % a][:].rearrange("p t g i s -> p (t g i s)"))

        def round_w4(copies):
            grouped = held("w4_grouped", [P, N // P, BLOCKS, RUN, SLOTS], BF16, "w1_grouped1", 2 * KIB)
            src = tiles["w4_raw"][:].rearrange("p s (t g i) -> p t g i s", t=N // P, i=RUN)
            for t, copy in enumerate(copies):
                copy(grouped[:, t], src[:, t])

        def stationary(name, a, t):
            if name == "size":
                return tiles["w3_codes"][:, t, a, :].bitcast(FP8X4), weight_plane("w3_planes", a, t)
            if name == "pred":
                return tiles["w2_codes"][:, t, a, :].bitcast(U8).bitcast(FP4X4), weight_plane("w2_planes", a, t)
            if (a, t) == (0, SLOTS - 1):
                return tiles["w1_last_codes"][:].bitcast(FP8X4), tiles["w1_last_scales"][:]
            cols = slice(t * P, (t + 1) * P)
            return tiles["w1_%d_codes" % a][:, cols].bitcast(FP8X4), tiles["w1_%d_scales" % a][:, cols]


        def product(name, number, j0, slots):
            width = SLOTS * CHUNK // len(slots)
            sums = bank(number, name)[:].rearrange("p (t j) -> p t j", j=width)
            for a in range(PASSES):
                for u, t in enumerate(slots):
                    codes, scale = stationary(name, a, t)
                    nc.tensor.matmul_mx(
                        out=sums[:, u, :],
                        lhsT=codes,
                        lhsT_scale=scale,
                        rhs=words(name, j0, width, a).bitcast(FP8X4),
                        rhs_scale=plane(name, a, j0, width),
                        start=(a == 0 and u == 0),
                        stop=(a == PASSES - 1 and u == len(slots) - 1),
                    )
            return sums.rearrange("p t j -> p j t")

        def size(pair, number, over, at):
            dst = held("factor%d" % pair, [P, 2, PAIR, 2], F32, over, at)
            for u in range(2):
                sums = product("size", number + u, pair * PAIR, (2 * u, 2 * u + 1))
                nc.scalar.activation(dst[:, u], sums, EXP)

        def pred(pair, number, over=None, at=0):
            dst = held("pred%d" % pair, [P, 2, PAIR, 2], F32, over, at)
            for u in range(2):
                nc.scalar.copy(dst[:, u], product("pred", number + u, pair * PAIR, (2 * u, 2 * u + 1)))

        def col(chunk, number):
            tiles["col%d" % chunk] = product("col", number, chunk * CHUNK, range(SLOTS))

        def smaller(chunk, over=None, at=0):
            dst = held("smaller%d" % chunk, [P, CHUNK, 2, 2], F32, over, at)[:]
            j0 = chunk % 2 * CHUNK
            other = tiles["pred%d" % (chunk // 2)][:, :, j0 : j0 + CHUNK, :].rearrange("p u j s -> p j u s")
            nc.vector.tensor_tensor(dst, tiles["col%d" % chunk].rearrange("p j (u s) -> p j u s", u=2), other, MIN)

        def times(engine, chunk):
            j0 = chunk % 2 * CHUNK
            dst = tiles["h%d" % (chunk // 2)][:, chunk % 2].rearrange("p j (u s) -> p j u s", u=2)
            factor = tiles["factor%d" % (chunk // 2)][:, :, j0 : j0 + CHUNK, :].rearrange("p u j s -> p j u s")
            engine.tensor_tensor(dst, tiles["smaller%d" % chunk][:], factor, MULT)

        def h_pair(pair, over=None, at=0, below=0, above=0):
            held("h%d" % pair, [P, 2, CHUNK, SLOTS], BF16, over, at, below, above)


        out_view = out.rearrange("(t p) j -> p t j", p=P)

        def quantize_h(chunk, count, over=None):
            h_part = tiles["h%d" % (chunk // 2)][:, chunk % 2 : chunk % 2 + count]
            quantize("hq%d" % chunk, h_part.rearrange("p u j t -> p (u j t)"), over)

        def head(chunk, count, numbers, stores=((0, 2, nc.sync), (2, 4, nc.sync))):
            width = count * CHUNK
            j0 = chunk * CHUNK
            group = N // P // len(numbers)
            sums = []
            for number in numbers:
                opened = bank(number, "last")
                for u in range(group):
                    cols = slice(len(sums) * P, (len(sums) + 1) * P)
                    sums.append(opened[:, u * width : (u + 1) * width])
                    nc.tensor.matmul_mx(
                        out=sums[-1],
                        lhsT=tiles["w4_codes"][:, cols].bitcast(FP8X4),
                        lhsT_scale=tiles["w4_scales"][:, cols],
                        rhs=tiles["hq%d_codes" % chunk][:].bitcast(FP8X4),
                        rhs_scale=tiles["hq%d_scales" % chunk][:],
                        start=True,
                        stop=True,
                    )
            for t0, t1, queue in stores:
                result = held("result%d_%d" % (chunk, t0), [P, t1 - t0, width], F32)
                for t in range(t0, t1):
                    nc.scalar.activation(result[:, t - t0, :], sums[t], EXP, bias=tiles["bias"][:, t : t + 1])
                queue.dma_start(out_view[:, t0:t1, j0 : j0 + width], result[:])

        clear_weight_scales("w2_scale_raw")
        load_table_scales()
        load_list("pred", offs2)
        load_list("size", offs3)
        load_list("col", offs)
        load_table(0)
        load_weight_scales(nc.sync, "w2_scale_raw", w2_scales)
        load_weight_words("w2_raw", H // 2, w2_words.rearrange("a p c -> p a c"))
        load_weight_words("w3_raw", H, w3_words.rearrange("a p c i -> p a (c i)"))
        for name in ("pred", "size", "col"):
            clear_planes(name)
        clear_weight_scales("w3_scale_raw")
        load_weight_scales(nc.gpsimd, "w3_scale_raw", w3_scales)
        reorder_scales(nc.scalar.copy, "w2_planes", "w2_scale_raw")
        reorder_words(nc.scalar.copy, "w2_codes", "w2_raw", RUN // 2)
        reorder_words(nc.scalar.copy, "w3_codes", "w3_raw", RUN)
        gather_scales("pred")
        place_planes("pred")
        load_table(1)
        load_w1(0)
        gather_scales("size")
        place_planes("size")
        gather_scales("col")
        load_w1(1, "scale_table", 64 - 8 * KIB)
        load_w4()
        place_planes("col")
        load_bias()

        gather_half("pred", 0, 0)
        gather_half("pred", 1, 0)
        gather_half("size", 0, 0)
        gather_pair("col", 0, 0)
        gather_pair("pred", 0, 1)
        gather_pair("pred", 1, 1)
        gather_half("pred", 1, 1)
        gather_half("size", 0, 1)
        pred(0, 0)
        pred(1, 2)
        gather_half("size", 1, 1)
        gather_half("size", 1, 0, over="words_pred_pair01")
        reorder_scales(nc.gpsimd.tensor_copy, "w3_planes", "w3_scale_raw")
        pred(2, 4)
        gather_pair("col", 0, 1, over="words_pred11")
        whole = slice(0, BLOCKS)
        round_w1(0, [(t, whole, pool_round) for t in range(3)])
        round_w1_last_slot("words_pred11", KIB)
        round_w1(1, [(t, whole, scalar_round) for t in range(SLOTS)], above=3 * KIB)
        quantize_w1(0)
        quantize("w1_last", tiles["w1_grouped_last"][:].rearrange("p g i s -> p (g i s)"))
        quantize_w1(1)
        size(0, 0, "w1_raw1", 64 - 4 * KIB)
        pred(3, 6, "w1_raw1", 64)
        gather_col(1, over="w1_raw1", at=64 + 4 * KIB)
        round_w4([pool_round, scalar_round, scalar_round, scalar_round])
        size(1, 2, "w4_raw", 64 - 4 * KIB)
        col(0, 0)
        col(1, 1)
        h_pair(0, below=2 * KIB, above=5 * KIB)
        smaller(0)
        times(nc.gpsimd, 0)
        smaller(1)
        times(nc.gpsimd, 1)
        col(2, 6)
        col(3, 7)
        gather_col(2, over="words_col_pair01")
        smaller(2)
        smaller(3)
        size(2, 4, "w4_raw", 64)
        size(3, 0, "w4_raw", 64 + 4 * KIB)
        quantize("w4", tiles["w4_grouped"][:].rearrange("p t g i s -> p (t g i s)"), over="smaller1")
        quantize_h(0, 2)
        col(4, 2)
        col(5, 3)
        head(0, 2, [6, 7])
        gather_col(3, over="h0", at=64 - 2 * KIB)
        h_pair(1, over="w4_grouped")
        times(nc.gpsimd, 2)
        times(nc.gpsimd, 3)
        smaller(4, over="w4_grouped", at=2 * KIB)
        smaller(5, over="h0", at=64)
        col(6, 4)
        col(7, 5)
        smaller(6)
        quantize_h(2, 2)
        head(2, 2, [0, 1])
        h_pair(2, over="factor1")
        h_pair(3, over="smaller3")
        times(nc.vector, 4)
        times(nc.vector, 5)
        quantize_h(4, 1)
        head(4, 1, [2, 3])
        times(nc.vector, 6)
        quantize_h(5, 1)
        head(5, 1, [4, 6])
        smaller(7, over="factor1", at=2 * KIB)
        quantize_h(6, 1)
        head(6, 1, [7, 0])
        times(nc.vector, 7)
        quantize_h(7, 1)
        head(7, 1, [1, 2, 3, 5], ((0, 2, nc.sync), (2, 3, nc.sync), (3, 4, nc.scalar)))
